import numpy as np
import ml_dtypes


def mxq(x, axis, fmt="e4m3"):
    dtype, down = {"e4m3": (ml_dtypes.float8_e4m3fn, 7), "e5m2": (ml_dtypes.float8_e5m2, 14)}[fmt]
    v = np.moveaxis(np.asarray(x, np.float32).astype(ml_dtypes.bfloat16).astype(np.float64), axis, -1)
    blocks = v.reshape(v.shape[:-1] + (-1, 32))
    amax = np.abs(blocks).max(-1, keepdims=True)
    byte = np.maximum(np.where(amax > 0, np.frexp(amax)[1] - 1 + 127, 0) - down, 1)
    scale = np.exp2(byte - 127.0)
    codes = (blocks / scale).astype(np.float32).astype(dtype).astype(np.float64)
    return np.moveaxis((codes * scale).reshape(v.shape), -1, axis)


WIDE = False


def mx_kscale(k):
    if not WIDE:
        return np.ones(k)
    levels = np.array([10, -10, 5, -5, 0])
    if k % 512:
        return np.exp2(np.random.permutation(np.resize(levels, k // 32))).repeat(32)
    a = np.empty((k // 512, 16))
    for p in range(k // 512):
        a[p, :8] = np.random.permutation(np.resize(levels, 8))
        for g in range(8):
            far = levels[np.abs(levels - a[p, g]) >= 10]
            a[p, g + 8] = far[np.random.randint(len(far))]
    return np.exp2(a.ravel()).repeat(32)


def f64(x):
    return np.asarray(x).astype(np.float64)


def striped(idx):
    return np.tile(idx.reshape(-1, 16).T, (8, 1)).astype(np.uint16)


def unstriped(offs):
    return offs[:16].T.reshape(-1).astype(np.int64)


E2M1 = np.array([0.0, 0.5, 1.0, 1.5, 2.0, 3.0, 4.0, 6.0, -0.0, -0.5, -1.0, -1.5, -2.0, -3.0, -4.0, -6.0])


def pack_weight(w, fmt):
    k, n = w.shape
    w = f64(np.asarray(w, np.float32).astype(ml_dtypes.bfloat16)).reshape(k // 32, 32, n)
    amax = np.abs(w).max(1)
    if fmt == "e4m3":
        byte = np.frexp(amax)[1] - 1 + 127 - 7
    else:
        mant, ex = np.frexp(amax / 6.0)
        byte = np.where(mant > 0.5, ex, ex - 1) + 127
    byte = np.clip(np.where(amax > 0, byte, 1), 1, 254)
    scaled = (w * np.exp2(127.0 - byte)[:, None, :]).reshape(k, n).astype(np.float32)
    by_word = np.ascontiguousarray(scaled.reshape(k // 512, 128, 4, n).transpose(0, 1, 3, 2))
    if fmt == "e4m3":
        words = by_word.astype(ml_dtypes.float8_e4m3fn).view(np.uint8)
    else:
        c = by_word.astype(ml_dtypes.float4_e2m1fn).view(np.uint8) & 0xF
        words = (c[..., 0::2] | (c[..., 1::2] << 4)).reshape(k // 512, 128, 2 * n)
    return np.ascontiguousarray(words), np.ascontiguousarray(byte.astype(np.uint8).reshape(k // 512, 16, n))


def unpack_weight(words, scales, fmt):
    g, _, n = scales.shape
    words = np.ascontiguousarray(words).reshape(g, 128, n, -1)
    if fmt == "e4m3":
        vals = words.view(ml_dtypes.float8_e4m3fn).astype(np.float64)
    else:
        nib = np.empty((g, 128, n, 4), np.uint8)
        nib[..., 0::2] = words & 0xF
        nib[..., 1::2] = words >> 4
        vals = E2M1[nib]
    vals = vals * np.repeat(np.exp2(scales.astype(np.float64) - 127.0), 8, axis=1)[..., None]
    return vals.transpose(0, 1, 3, 2).reshape(g * 512, n)


def gelu(v):
    return 0.5 * v * (1.0 + np.tanh(np.sqrt(2.0 / np.pi) * (v + 0.044715 * v**3)))


K, T, S, P, H = 1536, 2048, 1024, 512, 1024

def setup_inputs():
    n = np.random.standard_normal
    s = mx_kscale(K)[:, None]
    u = mx_kscale(H)[:, None]
    tab_words, tab_scales = pack_weight(n((K, T)) * s, "e4m3")
    wa_words, wa_scales = pack_weight(1.5 * n((H, H)) / np.sqrt(H) / u, "e2m1")
    return {
        "tab_words": tab_words, "tab_scales": tab_scales,
        "offs": striped(np.random.permutation(T)[:S]),
        "pos1": striped(np.random.permutation(S)[:P]),
        "pos2": striped(np.random.permutation(S)[:P]),
        "w1": (n((K, H)) / np.sqrt(K) / s).astype(np.float32),
        "gain": (1.2 * np.exp(0.3 * n(H)) * u[:, 0]).astype(np.float32),
        "wa_words": wa_words, "wa_scales": wa_scales,
        "wb": (1.5 * n((H, H)) / np.sqrt(H) / u).astype(np.float32),
        "sk": np.exp(0.3 * n(H)).astype(np.float32),
    }

def reference(tab_words, tab_scales, offs, pos1, pos2, w1, gain, wa_words, wa_scales, wb, sk):
    v = unpack_weight(tab_words, tab_scales, "e4m3")[:, unstriped(offs)]
    h = mxq(f64(w1), 0, "e4m3").T @ v
    x = h[:, unstriped(pos1)]
    z = mxq(x / (1.0 + np.exp(-x)) * f64(gain)[:, None], 0, "e4m3")
    ya = unpack_weight(wa_words, wa_scales, "e2m1").T @ z
    yb = mxq(f64(wb), 0, "e4m3").T @ z
    return np.maximum(ya, yb) - f64(sk)[:, None] * h[:, unstriped(pos2)]

@@ -1,0 +1,308 @@
+from contextlib import ExitStack
+
+import concourse.mybir as mybir
+
+K, T, S, M, H = 1536, 2048, 1024, 512, 1024
+FLOPS = 2 * K * H * S + 2 * 2 * H * H * M
+
+F32 = mybir.dt.float32
+BF16 = mybir.dt.bfloat16
+I32 = mybir.dt.int32
+U32 = mybir.dt.uint32
+U16 = mybir.dt.uint16
+U8 = mybir.dt.uint8
+FP8X4 = mybir.dt.float8_e4m3fn_x4
+FP4X4 = mybir.dt.float4_e2m1fn_x4
+ACT = mybir.ActivationFunctionType
+ALU = mybir.AluOpType
+
+P = 128
+PACK = 4
+KP = P * PACK
+BANK = 512
+KA = K // KP
+HB = H // KP
+SKIP_TAGS = (("stage1", "stage2"), ("zi0", "zi1"))
+LATE = 3
+ONV = ((0,0,0),(0,0,1),(1,0,0))
+
+
+def tile_list_mural_retouch_advice_kernel(tc, tab_words, tab_scales, offs, pos1, pos2, w1, gain,
+                                                    wa_words, wa_scales, wb, sk, out):
+    nc = tc.nc
+    with ExitStack() as ctx:
+        keep = ctx.enter_context(tc.tile_pool(name="keep", bufs=1))
+        ring = ctx.enter_context(tc.tile_pool(name="ring", bufs=3))
+        psum = ctx.enter_context(tc.psum_pool(name="psum", bufs=8))
+
+        offs_sb = keep.tile([P, S // 16], U16, name="offs_sb")
+        pos1_sb = keep.tile([P, M // 16], U16, name="pos1_sb")
+        pos2_sb = keep.tile([P, M // 16], U16, name="pos2_sb")
+        gain_sb = keep.tile([P, HB, PACK], F32, name="gain_sb")
+        sk_sb = keep.tile([P, HB, PACK], F32, name="sk_sb")
+        nsk_sb = keep.tile([P, HB, PACK], F32, name="nsk_sb")
+
+        tab_sc = keep.tile([P, T // 4], I32, name="tab_sc")
+        wa_sc_raw = keep.tile([P, HB, H // 4], I32, name="wa_sc_raw")
+        nc.vector.memset(tab_sc[:], 0)
+        nc.vector.memset(wa_sc_raw[:], 0)
+
+        tab_w = {}
+
+        def load_tab(a):
+            tab_w[a] = keep.tile([P, T], I32, name="tab_w%d" % a)
+            nc.sync.dma_start(out=tab_w[a][:], in_=tab_words[a].rearrange("p t i -> p (t i)").bitcast(I32))
+
+        raw = {}
+
+        def load_w(key, w, a, b, part=0, parts=1, tag=None):
+            width = KP // parts
+            if tag is None:
+                raw[key, part] = ring.tile([P, PACK, width], F32, name="raw", tag="raw", bufs=4)
+            else:
+                raw[key, part] = keep.tile([P, PACK, width], F32, name="raw", tag=tag)
+            c0 = b * KP + part * width
+            src = w[a * KP:(a + 1) * KP, c0:c0 + width].rearrange("(p j) c -> p j c", j=PACK)
+            nc.sync.dma_start(out=raw[key, part][:], in_=src)
+
+        grouped = {}
+
+        def cast_w(key, on_vector, part=0, parts=1):
+            if part == 0:
+                grouped[key] = ring.tile([P, PACK * KP], BF16, name="grouped", tag="grouped", align_bytes=64)
+            rows = P // parts
+            dst = grouped[key][:].rearrange("p (t m j) -> p m j t", t=PACK, j=PACK)[:, part * rows:(part + 1) * rows, :, :]
+            if (key, part) in raw and raw[key, part].shape[2] < KP:
+                src = raw[key, part][:].rearrange("p j (m t) -> p m j t", t=PACK)
+            else:
+                src = raw[key, 0][:].rearrange("p j (m t) -> p m j t", t=PACK)[:, part * rows:(part + 1) * rows, :, :]
+            if on_vector:
+                nc.vector.tensor_copy(out=dst, in_=src)
+            else:
+                nc.scalar.copy(out=dst, in_=src)
+
+        codes = {}
+        scales = {}
+
+        def quantize(key, src):
+            codes[key] = keep.tile([P, KP], U32, name="codes_%s%d%d" % key, align_bytes=64)
+            scales[key] = keep.tile([P, KP], U8, name="scales_%s%d%d" % key, align_bytes=64)
+            nc.vector.quantize_mx(out=codes[key][:].bitcast(FP8X4), scales=scales[key][:], in_=src)
+
+        def quant_w(key):
+            quantize(key, grouped[key][:])
+
+        warm = keep.tile([P, 8], F32, name="warm")
+        nc.gpsimd.memset(warm[:], 0.0)
+        nc.scalar.activation(warm[:], warm[:], ACT.Silu)
+        load_tab(0)
+        for q in range(4):
+            nc.sync.dma_start(out=tab_sc[32 * q: 32 * q + 4 * KA, :],
+                              in_=tab_scales[:, 4 * q: 4 * q + 4, :].bitcast(I32))
+        nc.sync.dma_start(offs_sb[:], offs)
+        wa_raw = keep.tile([P, HB, H // 2], I32, name="wa_raw")
+        nc.sync.dma_start(out=wa_raw[:], in_=wa_words.bitcast(I32).rearrange("a p c -> p a c"))
+        load_w(("w", 0, 0), w1, 0, 0)
+        for q in range(4):
+            nc.sync.dma_start(out=wa_sc_raw[32 * q: 32 * q + 4, :, :],
+                              in_=wa_scales[:, 4 * q: 4 * q + 4, :].bitcast(I32).rearrange("a r c -> r a c"))
+        load_w(("w", 1, 0), w1, 1, 0)
+        load_tab(1)
+        load_tab(2)
+        load_w(("w", 2, 0), w1, 2, 0, 0, 2)
+        load_w(("w", 2, 0), w1, 2, 0, 1, 2)
+        nc.sync.dma_start(pos1_sb[:], pos1)
+        load_w(("w", 0, 1), w1, 0, 1)
+        nc.sync.dma_start(pos2_sb[:], pos2)
+        nc.sync.dma_start(out=gain_sb[:], in_=gain.rearrange("(b p t) -> p b t", b=HB, t=PACK))
+        nc.sync.dma_start(out=sk_sb[:], in_=sk.rearrange("(b p t) -> p b t", b=HB, t=PACK))
+        load_w(("w", 1, 1), w1, 1, 1, tag="stage1")
+        load_w(("w", 2, 1), w1, 2, 1, tag="stage2")
+
+        v_sc = keep.tile([P, S], U8, name="v_sc", align_bytes=64)
+        nc.vector.tensor_copy(v_sc[:], tab_sc[:].bitcast(U8).indirect(offs_sb[:]))
+        v_w = {}
+
+        def gather_tab(a, u):
+            v_w[a, u] = keep.tile([P, BANK], U32, name="v_w%d%d" % (a, u), align_bytes=64)
+            cols = BANK // 16
+            nc.vector.tensor_copy(v_w[a, u][:], tab_w[a][:].bitcast(U32).indirect(offs_sb[:, u * cols:(u + 1) * cols]))
+
+        acc = {}
+
+        def stage1_pass(a, b, u, t):
+            if a == 0:
+                acc[b, u, t] = psum.tile([P, BANK], F32, name="acc", tag="acc")
+            key = ("w", a, b)
+            nc.tensor.matmul_mx(
+                out=acc[b, u, t][:],
+                lhsT=codes[key][:, t * P:(t + 1) * P].bitcast(FP8X4),
+                lhsT_scale=scales[key][:, t * P:(t + 1) * P],
+                rhs=v_w[a, u][:].bitcast(FP8X4),
+                rhs_scale=v_sc[4 * a:P, u * BANK:(u + 1) * BANK],
+                start=(a == 0), stop=(a == KA - 1))
+
+        h = {}
+
+        def evac_h(b, u, t):
+            if u == 0:
+                h[b, t] = keep.tile([P, S], F32, name="h%d%d" % (b, t))
+            nc.scalar.copy(out=h[b, t][:, u * BANK:(u + 1) * BANK], in_=acc[b, u, t][:])
+
+        gather_tab(0, 0)
+        gather_tab(0, 1)
+        cast_w(("w", 0, 0), False)
+        wa_w = keep.tile([P, HB * H * 2], U8, name="wa_w", align_bytes=64)
+        nc.vector.tensor_copy(
+            out=wa_w[:].bitcast(U16).rearrange("p (g t m) -> p g t m", t=PACK, m=P),
+            in_=wa_raw[:].rearrange("p a c -> p (a c)").bitcast(U16).rearrange("p (g m t) -> p g t m", t=PACK, m=P))
+        quant_w(("w", 0, 0))
+        wa_sc = keep.tile([P, HB * H], U8, name="wa_sc", align_bytes=64)
+        nc.vector.tensor_copy(
+            out=wa_sc[:].rearrange("p (g t m) -> p g t m", t=PACK, m=P),
+            in_=wa_sc_raw[:].rearrange("p a c -> p (a c)").bitcast(U8).rearrange("p (g m t) -> p g t m", t=PACK, m=P))
+        for u in range(2):
+            for t in range(PACK):
+                stage1_pass(0, 0, u, t)
+        cast_w(("w", 1, 0), False)
+        quant_w(("w", 1, 0))
+        gather_tab(1, 0)
+        gather_tab(1, 1)
+        for u in range(2):
+            for t in range(PACK):
+                stage1_pass(1, 0, u, t)
+        gather_tab(2, 0)
+        gather_tab(2, 1)
+        cast_w(("w", 2, 0), False, 0, 2)
+        cast_w(("w", 2, 0), True, 1, 2)
+        quant_w(("w", 2, 0))
+        for t in range(PACK):
+            for u in range(2):
+                stage1_pass(2, 0, u, t)
+        x = {}
+        skip = {}
+        zb = {}
+
+        def gather_x(b, t):
+            x[b, t] = keep.tile([P, M], F32, name="x%d%d" % (b, t), tag="x%d%d" % (b, t))
+            nc.vector.tensor_copy(x[b, t][:], h[b, t][:].indirect(pos1_sb[:]))
+
+        def gather_skip(b, t):
+            if b == 1:
+                tag = "zi1" if t >= LATE else "x1%d" % t
+                if t <= LATE:
+                    n = 1 if t < LATE else PACK - LATE
+                    pair = keep.tile([P, n, M], F32, name="skip_late", tag=tag, align_bytes=(64 if tag[0] == "z" else None))
+                    for i in range(n):
+                        skip[b, t + i] = pair[:, i, :]
+            elif t % 2 == 0:
+                pair = keep.tile([P, 2, M], F32, name="skip_late", tag=("stage1", "stage2")[t // 2])
+                skip[b, t], skip[b, t + 1] = pair[:, 0, :], pair[:, 1, :]
+            nc.vector.tensor_copy(skip[b, t], h[b, t][:].indirect(pos2_sb[:]))
+
+        def silu_gain(b, t):
+            if t == 0:
+                zb[b] = keep.tile([P, PACK, M], BF16, name="zb%d" % b)
+            act = ring.tile([P, M], F32, name="act", tag="act", bufs=2)
+            nc.scalar.activation(act[:], x[b, t][:], ACT.Silu)
+            nc.scalar.activation(zb[b][:, t, :], act[:], ACT.Copy, scale=gain_sb[:, b, t:t + 1])
+
+        zi = {}
+
+        def weave_z(b):
+            zi[b] = keep.tile([P, M * PACK], BF16, name="zi%d" % b, tag="zi%d" % b, align_bytes=64)
+            nc.vector.tensor_copy(out=zi[b][:].rearrange("p (c i t) -> p c t i", i=4, t=PACK),
+                                  in_=zb[b][:].rearrange("p t (c i) -> p c t i", i=4))
+
+        cast_w(("w", 0, 1), True)
+        quant_w(("w", 0, 1))
+        for b in range(HB):
+            for a in range(HB):
+                load_w(("b", a, b), wb, a, b)
+        for t in range(PACK):
+            evac_h(0, 0, t)
+            evac_h(0, 1, t)
+        for a in (1, 2):
+            cast_w(("w", a, 1), False)
+            quant_w(("w", a, 1))
+        for t in range(PACK):
+            for u in range(2):
+                for a in range(KA):
+                    stage1_pass(a, 1, u, t)
+        nc.vector.tensor_scalar(nsk_sb[:], sk_sb[:], -1.0, None, ALU.mult)
+        for b in range(HB):
+            for t in range(PACK):
+                if b == 1:
+                    evac_h(1, 0, t)
+                    evac_h(1, 1, t)
+                gather_x(b, t)
+            if b == 1:
+                pass
+            for t in range(PACK):
+                silu_gain(b, t)
+            weave_z(b)
+            quantize(("z", b, 0), zi[b][:])
+            if b == 0:
+                pass
+                for part in range(2):
+                    cast_w(("b", 0, 0), (0, 0, part) in ONV, part, 2)
+                quant_w(("b", 0, 0))
+                for part in range(2):
+                    cast_w(("b", 1, 0), (1, 0, part) in ONV, part, 2)
+                quant_w(("b", 1, 0))
+        for b in range(HB):
+            for t in range(PACK):
+                gather_skip(b, t)
+
+        ya = {}
+        yb = {}
+
+        def stage2_pass(a, b, t):
+            if a == 0:
+                ya[b, t] = psum.tile([P, M], F32, name="ya", tag="acc")
+                yb[b, t] = psum.tile([P, M], F32, name="yb", tag="acc")
+            z = ("z", a, 0)
+            col = a * H + b * KP + t * P
+            nc.tensor.matmul_mx(
+                out=ya[b, t][:], lhsT=wa_w[:, 2 * col:2 * (col + P)].bitcast(FP4X4), lhsT_scale=wa_sc[:, col:col + P],
+                rhs=codes[z][:].bitcast(FP8X4), rhs_scale=scales[z][:], start=(a == 0), stop=(a == HB - 1))
+            key = ("b", a, b)
+            nc.tensor.matmul_mx(
+                out=yb[b, t][:], lhsT=codes[key][:, t * P:(t + 1) * P].bitcast(FP8X4),
+                lhsT_scale=scales[key][:, t * P:(t + 1) * P],
+                rhs=codes[z][:].bitcast(FP8X4), rhs_scale=scales[z][:], start=(a == 0), stop=(a == HB - 1))
+
+        out_v = out.rearrange("(b p t) m -> b t p m", b=HB, t=PACK)
+        top = {}
+
+        def finish_max(b, t):
+            ya_sb = ring.tile([P, M], F32, name="ya_sb", tag="ya_sb", bufs=2)
+            nc.scalar.copy(out=ya_sb[:], in_=ya[b, t][:])
+            top[b, t] = ring.tile([P, M], F32, name="top", tag="top")
+            nc.vector.tensor_tensor(top[b, t][:], yb[b, t][:], ya_sb[:], ALU.max)
+
+        def finish_out(b, t):
+            res = ring.tile([P, M], F32, name="res", tag="res", bufs=6)
+            nc.vector.scalar_tensor_tensor(res[:], skip[b, t], nsk_sb[:, b, t:t + 1], top[b, t][:], ALU.mult, ALU.add)
+            nc.sync.dma_start(out=out_v[b, t], in_=res[:])
+
+        for a in range(HB):
+            for t in range(PACK):
+                stage2_pass(a, 0, t)
+        order = [(b, t) for b in range(HB) for t in range(PACK)]
+        for i, (b, t) in enumerate(order):
+            if i == 2:
+                pass
+                for part in range(2):
+                    cast_w(("b", 0, 1), (0, 1, part) in ONV, part, 2)
+                quant_w(("b", 0, 1))
+                for part in range(2):
+                    cast_w(("b", 1, 1), (1, 1, part) in ONV, part, 2)
+                quant_w(("b", 1, 1))
+            if b == 1:
+                for a in range(HB):
+                    stage2_pass(a, b, t)
+            finish_max(b, t)
+            if i > 0:
+                finish_out(*order[i - 1])
+        finish_out(*order[-1])

@@ -20,11 +20,11 @@ P = 128
 PACK = 4
 KP = P * PACK
 BANK = 512
-KA = K // KP
-HB = H // KP
-SKIP_TAGS = (("stage1", "stage2"), ("zi0", "zi1"))
-LATE = 3
-ONV = ((0,0,0),(0,0,1),(1,0,0))
+QUAD = 32
+K_PASSES = K // KP
+R_PASSES = H // KP
+HALVES = S // BANK
+OUT_TILES = H // P
 
 
 def tile_list_mural_retouch_advice_kernel(tc, tab_words, tab_scales, offs, pos1, pos2, w1, gain,
@@ -38,167 +38,82 @@ def tile_list_mural_retouch_advice_kernel(tc, tab_words, tab_scales, offs, pos1,
         offs_sb = keep.tile([P, S // 16], U16, name="offs_sb")
         pos1_sb = keep.tile([P, M // 16], U16, name="pos1_sb")
         pos2_sb = keep.tile([P, M // 16], U16, name="pos2_sb")
-        gain_sb = keep.tile([P, HB, PACK], F32, name="gain_sb")
-        sk_sb = keep.tile([P, HB, PACK], F32, name="sk_sb")
-        nsk_sb = keep.tile([P, HB, PACK], F32, name="nsk_sb")
-
+        gain_sb = keep.tile([P, R_PASSES, PACK], F32, name="gain_sb")
+        sk_sb = keep.tile([P, OUT_TILES], F32, name="sk_sb")
+        neg_sk = keep.tile([P, OUT_TILES], F32, name="neg_sk")
         tab_sc = keep.tile([P, T // 4], I32, name="tab_sc")
-        wa_sc_raw = keep.tile([P, HB, H // 4], I32, name="wa_sc_raw")
-        nc.vector.memset(tab_sc[:], 0)
-        nc.vector.memset(wa_sc_raw[:], 0)
-
-        tab_w = {}
+        wa_w = keep.tile([P, R_PASSES, 2 * H], U8, name="wa_w", align_bytes=64)
+        wa_sc = keep.tile([P, R_PASSES, H], U8, name="wa_sc", align_bytes=64)
+        v_sc = keep.tile([P, S], U8, name="v_sc", align_bytes=64)
+        tab_w, v_w, raw, grouped, codes, scales = {}, {}, {}, {}, {}, {}
+        acc, h, x, zb, zi, picked, skip, ya, yb, top = {}, {}, {}, {}, {}, {}, {}, {}, {}, {}
 
         def load_tab(a):
             tab_w[a] = keep.tile([P, T], I32, name="tab_w%d" % a)
             nc.sync.dma_start(out=tab_w[a][:], in_=tab_words[a].rearrange("p t i -> p (t i)").bitcast(I32))
 
-        raw = {}
-
-        def load_w(key, w, a, b, part=0, parts=1, tag=None):
-            width = KP // parts
+        def load_w(w, key, c0, width, tag=None):
+            a = key[1]
             if tag is None:
-                raw[key, part] = ring.tile([P, PACK, width], F32, name="raw", tag="raw", bufs=4)
+                tile = ring.tile([P, PACK, width], F32, name="raw", tag="raw", bufs=4)
             else:
-                raw[key, part] = keep.tile([P, PACK, width], F32, name="raw", tag=tag)
-            c0 = b * KP + part * width
-            src = w[a * KP:(a + 1) * KP, c0:c0 + width].rearrange("(p j) c -> p j c", j=PACK)
-            nc.sync.dma_start(out=raw[key, part][:], in_=src)
+                tile = keep.tile([P, PACK, width], F32, name="raw", tag=tag)
+            nc.sync.dma_start(out=tile[:], in_=w[a * KP:(a + 1) * KP, c0:c0 + width].rearrange("(p j) c -> p j c", j=PACK))
+            for part in range(width // (KP // 2)):
+                raw[key, (c0 % KP) // (KP // 2) + part] = tile[:, :, part * (KP // 2):(part + 1) * (KP // 2)]
+            raw[key] = tile[:]
 
-        grouped = {}
-
-        def cast_w(key, on_vector, part=0, parts=1):
-            if part == 0:
+        def cast(engine, key, part=None):
+            if key not in grouped:
                 grouped[key] = ring.tile([P, PACK * KP], BF16, name="grouped", tag="grouped", align_bytes=64)
-            rows = P // parts
-            dst = grouped[key][:].rearrange("p (t m j) -> p m j t", t=PACK, j=PACK)[:, part * rows:(part + 1) * rows, :, :]
-            if (key, part) in raw and raw[key, part].shape[2] < KP:
-                src = raw[key, part][:].rearrange("p j (m t) -> p m j t", t=PACK)
+            if key[0] == "w":
+                dst = grouped[key][:].rearrange("p (t m j) -> p m j t", t=PACK, j=PACK)
+                order = "p j (m t) -> p m j t"
             else:
-                src = raw[key, 0][:].rearrange("p j (m t) -> p m j t", t=PACK)[:, part * rows:(part + 1) * rows, :, :]
-            if on_vector:
+                dst = grouped[key][:].rearrange("p (m t j) -> p m j t", t=PACK, j=PACK)
+                order = "p j (m t) -> p m j t"
+            if part is None:
+                src = raw[key].rearrange(order, t=PACK)
+            else:
+                dst = dst[:, part * (P // 2):(part + 1) * (P // 2), :, :]
+                src = raw[key, part].rearrange(order, t=PACK)
+            if engine == "vector":
                 nc.vector.tensor_copy(out=dst, in_=src)
+            elif engine == "gpsimd":
+                nc.gpsimd.tensor_scalar(dst, src, 1.0, 0.0, ALU.mult, ALU.add)
             else:
                 nc.scalar.copy(out=dst, in_=src)
-
-        codes = {}
-        scales = {}
 
         def quantize(key, src):
             codes[key] = keep.tile([P, KP], U32, name="codes_%s%d%d" % key, align_bytes=64)
             scales[key] = keep.tile([P, KP], U8, name="scales_%s%d%d" % key, align_bytes=64)
-            nc.vector.quantize_mx(out=codes[key][:].bitcast(FP8X4), scales=scales[key][:], in_=src)
-
-        def quant_w(key):
-            quantize(key, grouped[key][:])
-
-        warm = keep.tile([P, 8], F32, name="warm")
-        nc.gpsimd.memset(warm[:], 0.0)
-        nc.scalar.activation(warm[:], warm[:], ACT.Silu)
-        load_tab(0)
-        for q in range(4):
-            nc.sync.dma_start(out=tab_sc[32 * q: 32 * q + 4 * KA, :],
-                              in_=tab_scales[:, 4 * q: 4 * q + 4, :].bitcast(I32))
-        nc.sync.dma_start(offs_sb[:], offs)
-        wa_raw = keep.tile([P, HB, H // 2], I32, name="wa_raw")
-        nc.sync.dma_start(out=wa_raw[:], in_=wa_words.bitcast(I32).rearrange("a p c -> p a c"))
-        load_w(("w", 0, 0), w1, 0, 0)
-        for q in range(4):
-            nc.sync.dma_start(out=wa_sc_raw[32 * q: 32 * q + 4, :, :],
-                              in_=wa_scales[:, 4 * q: 4 * q + 4, :].bitcast(I32).rearrange("a r c -> r a c"))
-        load_w(("w", 1, 0), w1, 1, 0)
-        load_tab(1)
-        load_tab(2)
-        load_w(("w", 2, 0), w1, 2, 0, 0, 2)
-        load_w(("w", 2, 0), w1, 2, 0, 1, 2)
-        nc.sync.dma_start(pos1_sb[:], pos1)
-        load_w(("w", 0, 1), w1, 0, 1)
-        nc.sync.dma_start(pos2_sb[:], pos2)
-        nc.sync.dma_start(out=gain_sb[:], in_=gain.rearrange("(b p t) -> p b t", b=HB, t=PACK))
-        nc.sync.dma_start(out=sk_sb[:], in_=sk.rearrange("(b p t) -> p b t", b=HB, t=PACK))
-        load_w(("w", 1, 1), w1, 1, 1, tag="stage1")
-        load_w(("w", 2, 1), w1, 2, 1, tag="stage2")
-
-        v_sc = keep.tile([P, S], U8, name="v_sc", align_bytes=64)
-        nc.vector.tensor_copy(v_sc[:], tab_sc[:].bitcast(U8).indirect(offs_sb[:]))
-        v_w = {}
+            nc.vector.quantize_mx(out=codes[key][:].bitcast(FP8X4), scales=scales[key][:], in_=src[:])
 
         def gather_tab(a, u):
             v_w[a, u] = keep.tile([P, BANK], U32, name="v_w%d%d" % (a, u), align_bytes=64)
             cols = BANK // 16
             nc.vector.tensor_copy(v_w[a, u][:], tab_w[a][:].bitcast(U32).indirect(offs_sb[:, u * cols:(u + 1) * cols]))
 
-        acc = {}
-
-        def stage1_pass(a, b, u, t):
+        def encoder_pass(a, b, t, u):
             if a == 0:
-                acc[b, u, t] = psum.tile([P, BANK], F32, name="acc", tag="acc")
+                acc[b, t, u] = psum.tile([P, BANK], F32, name="acc", tag="bank")
             key = ("w", a, b)
             nc.tensor.matmul_mx(
-                out=acc[b, u, t][:],
+                out=acc[b, t, u][:],
                 lhsT=codes[key][:, t * P:(t + 1) * P].bitcast(FP8X4),
                 lhsT_scale=scales[key][:, t * P:(t + 1) * P],
                 rhs=v_w[a, u][:].bitcast(FP8X4),
                 rhs_scale=v_sc[4 * a:P, u * BANK:(u + 1) * BANK],
-                start=(a == 0), stop=(a == KA - 1))
+                start=(a == 0), stop=(a == K_PASSES - 1))
 
-        h = {}
-
-        def evac_h(b, u, t):
-            if u == 0:
-                h[b, t] = keep.tile([P, S], F32, name="h%d%d" % (b, t))
-            nc.scalar.copy(out=h[b, t][:, u * BANK:(u + 1) * BANK], in_=acc[b, u, t][:])
-
-        gather_tab(0, 0)
-        gather_tab(0, 1)
-        cast_w(("w", 0, 0), False)
-        wa_w = keep.tile([P, HB * H * 2], U8, name="wa_w", align_bytes=64)
-        nc.vector.tensor_copy(
-            out=wa_w[:].bitcast(U16).rearrange("p (g t m) -> p g t m", t=PACK, m=P),
-            in_=wa_raw[:].rearrange("p a c -> p (a c)").bitcast(U16).rearrange("p (g m t) -> p g t m", t=PACK, m=P))
-        quant_w(("w", 0, 0))
-        wa_sc = keep.tile([P, HB * H], U8, name="wa_sc", align_bytes=64)
-        nc.vector.tensor_copy(
-            out=wa_sc[:].rearrange("p (g t m) -> p g t m", t=PACK, m=P),
-            in_=wa_sc_raw[:].rearrange("p a c -> p (a c)").bitcast(U8).rearrange("p (g m t) -> p g t m", t=PACK, m=P))
-        for u in range(2):
-            for t in range(PACK):
-                stage1_pass(0, 0, u, t)
-        cast_w(("w", 1, 0), False)
-        quant_w(("w", 1, 0))
-        gather_tab(1, 0)
-        gather_tab(1, 1)
-        for u in range(2):
-            for t in range(PACK):
-                stage1_pass(1, 0, u, t)
-        gather_tab(2, 0)
-        gather_tab(2, 1)
-        cast_w(("w", 2, 0), False, 0, 2)
-        cast_w(("w", 2, 0), True, 1, 2)
-        quant_w(("w", 2, 0))
-        for t in range(PACK):
-            for u in range(2):
-                stage1_pass(2, 0, u, t)
-        x = {}
-        skip = {}
-        zb = {}
+        def fetch_h(b, t):
+            h[b, t] = keep.tile([P, S], F32, name="h%d%d" % (b, t))
+            for u in range(HALVES):
+                nc.scalar.copy(out=h[b, t][:, u * BANK:(u + 1) * BANK], in_=acc[b, t, u][:])
 
         def gather_x(b, t):
             x[b, t] = keep.tile([P, M], F32, name="x%d%d" % (b, t), tag="x%d%d" % (b, t))
             nc.vector.tensor_copy(x[b, t][:], h[b, t][:].indirect(pos1_sb[:]))
-
-        def gather_skip(b, t):
-            if b == 1:
-                tag = "zi1" if t >= LATE else "x1%d" % t
-                if t <= LATE:
-                    n = 1 if t < LATE else PACK - LATE
-                    pair = keep.tile([P, n, M], F32, name="skip_late", tag=tag, align_bytes=(64 if tag[0] == "z" else None))
-                    for i in range(n):
-                        skip[b, t + i] = pair[:, i, :]
-            elif t % 2 == 0:
-                pair = keep.tile([P, 2, M], F32, name="skip_late", tag=("stage1", "stage2")[t // 2])
-                skip[b, t], skip[b, t + 1] = pair[:, 0, :], pair[:, 1, :]
-            nc.vector.tensor_copy(skip[b, t], h[b, t][:].indirect(pos2_sb[:]))
 
         def silu_gain(b, t):
             if t == 0:
@@ -207,102 +122,149 @@ def tile_list_mural_retouch_advice_kernel(tc, tab_words, tab_scales, offs, pos1,
             nc.scalar.activation(act[:], x[b, t][:], ACT.Silu)
             nc.scalar.activation(zb[b][:, t, :], act[:], ACT.Copy, scale=gain_sb[:, b, t:t + 1])
 
-        zi = {}
-
-        def weave_z(b):
+        def make_z(b):
             zi[b] = keep.tile([P, M * PACK], BF16, name="zi%d" % b, tag="zi%d" % b, align_bytes=64)
             nc.vector.tensor_copy(out=zi[b][:].rearrange("p (c i t) -> p c t i", i=4, t=PACK),
                                   in_=zb[b][:].rearrange("p t (c i) -> p c t i", i=4))
+            quantize(("z", b, 0), zi[b])
 
-        cast_w(("w", 0, 1), True)
-        quant_w(("w", 0, 1))
-        for b in range(HB):
-            for a in range(HB):
-                load_w(("b", a, b), wb, a, b)
+        def gather_skip(b, t, dst):
+            nc.vector.tensor_copy(dst, h[b, t][:].indirect(pos2_sb[:]))
+            for q in range(P // QUAD):
+                n = PACK * b + q
+                if t == 0:
+                    skip[n] = keep.tile([P, M], F32, name="skip%d" % n)
+                nc.sync.dma_start(out=skip[n][t:P:PACK, :], in_=dst[q * QUAD:(q + 1) * QUAD, :])
+
+        def product_pass(a, n):
+            if a == 0:
+                ya[n] = psum.tile([P, M], F32, name="ya", tag="bank")
+                yb[n] = psum.tile([P, M], F32, name="yb", tag="bank")
+            z = ("z", a, 0)
+            nc.tensor.matmul_mx(
+                out=ya[n][:], lhsT=wa_w[:, a, 2 * n * P:2 * (n + 1) * P].bitcast(FP4X4),
+                lhsT_scale=wa_sc[:, a, n * P:(n + 1) * P],
+                rhs=codes[z][:].bitcast(FP8X4), rhs_scale=scales[z][:], start=(a == 0), stop=(a == R_PASSES - 1))
+            key, c = ("b", a, n // PACK), n % PACK
+            nc.tensor.matmul_mx(
+                out=yb[n][:], lhsT=codes[key][:, c * P:(c + 1) * P].bitcast(FP8X4),
+                lhsT_scale=scales[key][:, c * P:(c + 1) * P],
+                rhs=codes[z][:].bitcast(FP8X4), rhs_scale=scales[z][:], start=(a == 0), stop=(a == R_PASSES - 1))
+
+        def larger(n):
+            ya_sb = ring.tile([P, M], F32, name="ya_sb", tag="ya_sb", bufs=2)
+            nc.scalar.copy(out=ya_sb[:], in_=ya[n][:])
+            top[n] = ring.tile([P, M], F32, name="top", tag="top")
+            nc.vector.tensor_tensor(top[n][:], yb[n][:], ya_sb[:], ALU.max)
+
+        def finish(n, c0=0, c1=M):
+            nc.vector.scalar_tensor_tensor(skip[n][:, c0:c1], skip[n][:, c0:c1], neg_sk[:, n:n + 1], top[n][:, c0:c1],
+                                           ALU.mult, ALU.add)
+            nc.sync.dma_start(out=out[n * P:(n + 1) * P, c0:c1], in_=skip[n][:, c0:c1])
+
+        nc.vector.memset(tab_sc[:], 0)
+        nc.vector.memset(wa_sc[:].bitcast(I32), 0)
+        warm = keep.tile([P, 8], F32, name="warm")
+        nc.gpsimd.memset(warm[:], 0.0)
+        nc.scalar.activation(warm[:], warm[:], ACT.Silu)
+
+        nc.sync.dma_start(offs_sb[:], offs)
+        load_tab(0)
+        load_w(w1, ("w", 0, 0), 0, KP)
+        for q in range(4):
+            nc.sync.dma_start(out=tab_sc[QUAD * q:QUAD * q + 4 * K_PASSES, :],
+                              in_=tab_scales[:, 4 * q:4 * q + 4, :].bitcast(I32))
+        load_tab(1)
+        load_w(w1, ("w", 1, 0), 0, KP)
+        load_tab(2)
+        load_w(w1, ("w", 2, 0), 0, KP // 2, tag="half0")
+        load_w(w1, ("w", 2, 0), KP // 2, KP // 2, tag="half1")
+        nc.sync.dma_start(pos1_sb[:], pos1)
+        load_w(w1, ("w", 0, 1), KP, KP)
+        load_w(w1, ("w", 1, 1), KP, KP, tag="late1")
+        load_w(w1, ("w", 2, 1), KP, KP, tag="late2")
+        nc.sync.dma_start(pos2_sb[:], pos2)
+        nc.sync.dma_start(out=gain_sb[:], in_=gain.rearrange("(b p t) -> p b t", b=R_PASSES, t=PACK))
+
+        for u in range(HALVES):
+            gather_tab(0, u)
+        nc.vector.tensor_copy(v_sc[:], tab_sc[:].bitcast(U8).indirect(offs_sb[:]))
+        for a in range(K_PASSES):
+            if a > 0:
+                for u in range(HALVES):
+                    gather_tab(a, u)
+            if a < K_PASSES - 1:
+                cast("scalar", ("w", a, 0))
+            else:
+                cast("scalar", ("w", a, 0), 0)
+                cast("vector", ("w", a, 0), 1)
+            quantize(("w", a, 0), grouped["w", a, 0])
+            for t in range(PACK):
+                for u in range(HALVES):
+                    encoder_pass(a, 0, t, u)
+
+        cast("vector", ("w", 0, 1))
+        quantize(("w", 0, 1), grouped["w", 0, 1])
+        load_w(wb, ("b", 0, 0), 0, KP)
+        nc.sync.dma_start(out=wa_w[:].bitcast(I32), in_=wa_words.bitcast(I32).rearrange("a p c -> p a c"))
+        for q in range(4):
+            nc.sync.dma_start(out=wa_sc[QUAD * q:QUAD * q + 4, :, :].bitcast(I32),
+                              in_=wa_scales[:, 4 * q:4 * q + 4, :].bitcast(I32).rearrange("a r c -> r a c"))
+        load_w(wb, ("b", 1, 0), 0, KP)
+        load_w(wb, ("b", 0, 1), KP, KP)
+        load_w(wb, ("b", 1, 1), KP, KP)
+        with nc.allow_non_contiguous_dma(reason="one skip factor for each output row, one row to a partition"):
+            nc.sync.dma_start(out=sk_sb[:], in_=sk.rearrange("(n p) -> p n", p=P))
         for t in range(PACK):
-            evac_h(0, 0, t)
-            evac_h(0, 1, t)
-        for a in (1, 2):
-            cast_w(("w", a, 1), False)
-            quant_w(("w", a, 1))
+            fetch_h(0, t)
+        for a in range(1, K_PASSES):
+            cast("scalar" if a == 1 else "scalar", ("w", a, 1))
+            quantize(("w", a, 1), grouped["w", a, 1])
         for t in range(PACK):
-            for u in range(2):
-                for a in range(KA):
-                    stage1_pass(a, 1, u, t)
-        nc.vector.tensor_scalar(nsk_sb[:], sk_sb[:], -1.0, None, ALU.mult)
-        for b in range(HB):
+            for u in range(HALVES):
+                for a in range(K_PASSES):
+                    encoder_pass(a, 1, t, u)
+        nc.vector.tensor_scalar(neg_sk[:], sk_sb[:], -1.0, None, ALU.mult)
+
+        def cast_wb(a, b):
+            for part in range(2):
+                cast("vector" if (a, b, part) in ((0, 0, 0), (0, 0, 1)) else "scalar", ("b", a, b), part)
+            quantize(("b", a, b), grouped["b", a, b])
+
+        for b in range(R_PASSES):
             for t in range(PACK):
                 if b == 1:
-                    evac_h(1, 0, t)
-                    evac_h(1, 1, t)
+                    fetch_h(1, t)
                 gather_x(b, t)
-            if b == 1:
-                pass
             for t in range(PACK):
                 silu_gain(b, t)
-            weave_z(b)
-            quantize(("z", b, 0), zi[b][:])
+            make_z(b)
             if b == 0:
-                pass
-                for part in range(2):
-                    cast_w(("b", 0, 0), (0, 0, part) in ONV, part, 2)
-                quant_w(("b", 0, 0))
-                for part in range(2):
-                    cast_w(("b", 1, 0), (1, 0, part) in ONV, part, 2)
-                quant_w(("b", 1, 0))
-        for b in range(HB):
-            for t in range(PACK):
-                gather_skip(b, t)
+                cast_wb(0, 0)
+                cast_wb(1, 0)
+        for pair in range(2):
+            held = keep.tile([P, 2, M], F32, name="held_late", tag="late%d" % (pair + 1))
+            for i in range(2):
+                gather_skip(0, 2 * pair + i, held[:, i, :])
+        for t in range(PACK):
+            if t < 3:
+                held = keep.tile([P, M], F32, name="held", tag="x1%d" % t)
+            else:
+                held = keep.tile([P, M], F32, name="held", tag="zi%d" % (t - 2), align_bytes=64)
+            gather_skip(1, t, held[:])
 
-        ya = {}
-        yb = {}
-
-        def stage2_pass(a, b, t):
-            if a == 0:
-                ya[b, t] = psum.tile([P, M], F32, name="ya", tag="acc")
-                yb[b, t] = psum.tile([P, M], F32, name="yb", tag="acc")
-            z = ("z", a, 0)
-            col = a * H + b * KP + t * P
-            nc.tensor.matmul_mx(
-                out=ya[b, t][:], lhsT=wa_w[:, 2 * col:2 * (col + P)].bitcast(FP4X4), lhsT_scale=wa_sc[:, col:col + P],
-                rhs=codes[z][:].bitcast(FP8X4), rhs_scale=scales[z][:], start=(a == 0), stop=(a == HB - 1))
-            key = ("b", a, b)
-            nc.tensor.matmul_mx(
-                out=yb[b, t][:], lhsT=codes[key][:, t * P:(t + 1) * P].bitcast(FP8X4),
-                lhsT_scale=scales[key][:, t * P:(t + 1) * P],
-                rhs=codes[z][:].bitcast(FP8X4), rhs_scale=scales[z][:], start=(a == 0), stop=(a == HB - 1))
-
-        out_v = out.rearrange("(b p t) m -> b t p m", b=HB, t=PACK)
-        top = {}
-
-        def finish_max(b, t):
-            ya_sb = ring.tile([P, M], F32, name="ya_sb", tag="ya_sb", bufs=2)
-            nc.scalar.copy(out=ya_sb[:], in_=ya[b, t][:])
-            top[b, t] = ring.tile([P, M], F32, name="top", tag="top")
-            nc.vector.tensor_tensor(top[b, t][:], yb[b, t][:], ya_sb[:], ALU.max)
-
-        def finish_out(b, t):
-            res = ring.tile([P, M], F32, name="res", tag="res", bufs=6)
-            nc.vector.scalar_tensor_tensor(res[:], skip[b, t], nsk_sb[:, b, t:t + 1], top[b, t][:], ALU.mult, ALU.add)
-            nc.sync.dma_start(out=out_v[b, t], in_=res[:])
-
-        for a in range(HB):
-            for t in range(PACK):
-                stage2_pass(a, 0, t)
-        order = [(b, t) for b in range(HB) for t in range(PACK)]
-        for i, (b, t) in enumerate(order):
-            if i == 2:
-                pass
-                for part in range(2):
-                    cast_w(("b", 0, 1), (0, 1, part) in ONV, part, 2)
-                quant_w(("b", 0, 1))
-                for part in range(2):
-                    cast_w(("b", 1, 1), (1, 1, part) in ONV, part, 2)
-                quant_w(("b", 1, 1))
-            if b == 1:
-                for a in range(HB):
-                    stage2_pass(a, b, t)
-            finish_max(b, t)
-            if i > 0:
-                finish_out(*order[i - 1])
-        finish_out(*order[-1])
+        for a in range(R_PASSES):
+            for n in range(PACK):
+                product_pass(a, n)
+        for n in range(OUT_TILES):
+            if n == 2:
+                cast_wb(0, 1)
+                cast_wb(1, 1)
+            if n >= PACK:
+                for a in range(R_PASSES):
+                    product_pass(a, n)
+            larger(n)
+            if n > 0:
+                finish(n - 1)
+        finish(OUT_TILES - 1, 0, M // 2)
+        finish(OUT_TILES - 1, M // 2, M)

@@ -1,6 +1,7 @@
 from contextlib import ExitStack
 
 import concourse.mybir as mybir
+from concourse.masks import make_identity
 
 K, T, S, M, H = 1536, 2048, 1024, 512, 1024
 FLOPS = 2 * K * H * S + 2 * 2 * H * H * M
@@ -24,11 +25,14 @@ QUAD = 32
 K_PASSES = K // KP
 R_PASSES = H // KP
 HALVES = S // BANK
-OUT_TILES = H // P
+TILES = H // P
+GROUP = 2 * P
+GROUPS = H // GROUP
+ON_SCALAR = ((0, 1), (0, 2))
 
 
 def tile_list_mural_retouch_advice_kernel(tc, tab_words, tab_scales, offs, pos1, pos2, w1, gain,
-                                                    wa_words, wa_scales, wb, sk, out):
+                                                        wa_words, wa_scales, wb, sk, out):
     nc = tc.nc
     with ExitStack() as ctx:
         keep = ctx.enter_context(tc.tile_pool(name="keep", bufs=1))
@@ -38,103 +42,106 @@ def tile_list_mural_retouch_advice_kernel(tc, tab_words, tab_scales, offs, pos1,
         offs_sb = keep.tile([P, S // 16], U16, name="offs_sb")
         pos1_sb = keep.tile([P, M // 16], U16, name="pos1_sb")
         pos2_sb = keep.tile([P, M // 16], U16, name="pos2_sb")
-        gain_sb = keep.tile([P, R_PASSES, PACK], F32, name="gain_sb")
-        sk_sb = keep.tile([P, OUT_TILES], F32, name="sk_sb")
-        neg_sk = keep.tile([P, OUT_TILES], F32, name="neg_sk")
+        rows = keep.tile([P, P], F32, name="rows")
+        ident = keep.tile([P, P], F32, name="ident")
+        gain_sb = keep.tile([P, TILES], F32, name="gain_sb")
+        neg_sk = keep.tile([P, TILES], F32, name="neg_sk")
         tab_sc = keep.tile([P, T // 4], I32, name="tab_sc")
         wa_w = keep.tile([P, R_PASSES, 2 * H], U8, name="wa_w", align_bytes=64)
         wa_sc = keep.tile([P, R_PASSES, H], U8, name="wa_sc", align_bytes=64)
         v_sc = keep.tile([P, S], U8, name="v_sc", align_bytes=64)
         tab_w, v_w, raw, grouped, codes, scales = {}, {}, {}, {}, {}, {}
-        acc, h, x, zb, zi, picked, skip, ya, yb, top = {}, {}, {}, {}, {}, {}, {}, {}, {}, {}
+        acc, h, x, act, zb, zp, zi, skip, ya, yb, top = {}, {}, {}, {}, {}, {}, {}, {}, {}, {}, {}
 
         def load_tab(a):
-            tab_w[a] = keep.tile([P, T], I32, name="tab_w%d" % a)
+            tab_w[a] = keep.tile([P, T], I32, name="tab_w%d" % a, tag="big%d" % a, align_bytes=64)
             nc.sync.dma_start(out=tab_w[a][:], in_=tab_words[a].rearrange("p t i -> p (t i)").bitcast(I32))
 
-        def load_w(w, key, c0, width, tag=None):
-            a = key[1]
-            if tag is None:
-                tile = ring.tile([P, PACK, width], F32, name="raw", tag="raw", bufs=4)
-            else:
-                tile = keep.tile([P, PACK, width], F32, name="raw", tag=tag)
-            nc.sync.dma_start(out=tile[:], in_=w[a * KP:(a + 1) * KP, c0:c0 + width].rearrange("(p j) c -> p j c", j=PACK))
-            for part in range(width // (KP // 2)):
-                raw[key, (c0 % KP) // (KP // 2) + part] = tile[:, :, part * (KP // 2):(part + 1) * (KP // 2)]
-            raw[key] = tile[:]
+        def load_w(w, name, a, g, groups, tag):
+            tile = keep.tile([P, PACK, groups * GROUP], F32, name="raw", tag=tag, align_bytes=64)
+            nc.sync.dma_start(out=tile[:], in_=w[a * KP:(a + 1) * KP, g * GROUP:(g + groups) * GROUP]
+                              .rearrange("(p j) c -> p j c", j=PACK))
+            for e in range(groups):
+                raw[name, a, g + e] = tile[:, :, e * GROUP:(e + 1) * GROUP]
 
-        def cast(engine, key, part=None):
-            if key not in grouped:
-                grouped[key] = ring.tile([P, PACK * KP], BF16, name="grouped", tag="grouped", align_bytes=64)
+        def load_w1(a, g, groups=1):
+            load_w(w1, "w", a, g, groups, "raw%d%d" % (a, g))
+
+        def cast(engine, key):
             if key[0] == "w":
-                dst = grouped[key][:].rearrange("p (t m j) -> p m j t", t=PACK, j=PACK)
-                order = "p j (m t) -> p m j t"
+                grouped[key] = ring.tile([P, PACK * GROUP], BF16, name="grouped", tag="grouped", bufs=4, align_bytes=64)
             else:
-                dst = grouped[key][:].rearrange("p (m t j) -> p m j t", t=PACK, j=PACK)
-                order = "p j (m t) -> p m j t"
-            if part is None:
-                src = raw[key].rearrange(order, t=PACK)
-            else:
-                dst = dst[:, part * (P // 2):(part + 1) * (P // 2), :, :]
-                src = raw[key, part].rearrange(order, t=PACK)
+                tag = ("x6", "act0", "x7", "act1")[(R_PASSES * key[2] + key[1]) % 4]
+                grouped[key] = keep.tile([P, PACK * GROUP], BF16, name="grouped_b", tag=tag, align_bytes=64)
+            dst = grouped[key][:].rearrange("p (m i j) -> p m j i", i=4, j=PACK)
+            src = raw[key].rearrange("p j (m i) -> p m j i", i=4)
             if engine == "vector":
                 nc.vector.tensor_copy(out=dst, in_=src)
-            elif engine == "gpsimd":
-                nc.gpsimd.tensor_scalar(dst, src, 1.0, 0.0, ALU.mult, ALU.add)
             else:
                 nc.scalar.copy(out=dst, in_=src)
 
-        def quantize(key, src):
-            codes[key] = keep.tile([P, KP], U32, name="codes_%s%d%d" % key, align_bytes=64)
-            scales[key] = keep.tile([P, KP], U8, name="scales_%s%d%d" % key, align_bytes=64)
-            nc.vector.quantize_mx(out=codes[key][:].bitcast(FP8X4), scales=scales[key][:], in_=src[:])
+        def quantize(key, src, width):
+            codes[key] = keep.tile([P, width], U32, name="codes_%s%d%d" % key, align_bytes=64)
+            if key not in scales:
+                scales[key] = keep.tile([P, width], U8, name="scales_%s%d%d" % key, align_bytes=64)[:]
+            nc.vector.quantize_mx(out=codes[key][:].bitcast(FP8X4), scales=scales[key], in_=src[:])
 
-        def gather_tab(a, u):
-            v_w[a, u] = keep.tile([P, BANK], U32, name="v_w%d%d" % (a, u), align_bytes=64)
-            cols = BANK // 16
-            nc.vector.tensor_copy(v_w[a, u][:], tab_w[a][:].bitcast(U32).indirect(offs_sb[:, u * cols:(u + 1) * cols]))
+        def weights(key, engine):
+            cast(engine, key)
+            quantize(key, grouped[key], GROUP)
 
-        def encoder_pass(a, b, t, u):
+        def gather_tab(a, pieces):
+            v_w[a] = keep.tile([P, S], U32, name="v_w%d" % a, align_bytes=64)
+            n = S // pieces
+            for u in range(pieces):
+                nc.vector.tensor_copy(v_w[a][:, u * n:(u + 1) * n],
+                                      tab_w[a][:].bitcast(U32).indirect(offs_sb[:, u * n // 16:(u + 1) * n // 16]))
+
+        def encoder_pass(a, j, u):
             if a == 0:
-                acc[b, t, u] = psum.tile([P, BANK], F32, name="acc", tag="bank")
-            key = ("w", a, b)
+                acc[j, u] = psum.tile([P, BANK], F32, name="acc", tag="bank")
+            key, c = ("w", a, j // 2), j % 2
             nc.tensor.matmul_mx(
-                out=acc[b, t, u][:],
-                lhsT=codes[key][:, t * P:(t + 1) * P].bitcast(FP8X4),
-                lhsT_scale=scales[key][:, t * P:(t + 1) * P],
-                rhs=v_w[a, u][:].bitcast(FP8X4),
+                out=acc[j, u][:],
+                lhsT=codes[key][:, c * P:(c + 1) * P].bitcast(FP8X4),
+                lhsT_scale=scales[key][:, c * P:(c + 1) * P],
+                rhs=v_w[a][:, u * BANK:(u + 1) * BANK].bitcast(FP8X4),
                 rhs_scale=v_sc[4 * a:P, u * BANK:(u + 1) * BANK],
                 start=(a == 0), stop=(a == K_PASSES - 1))
 
-        def fetch_h(b, t):
-            h[b, t] = keep.tile([P, S], F32, name="h%d%d" % (b, t))
+        def encoder(a, g):
+            for j in (2 * g, 2 * g + 1):
+                for u in range(HALVES):
+                    encoder_pass(a, j, u)
+
+        def fetch_h(j):
+            h[j] = keep.tile([P, S], F32, name="h%d" % j)
             for u in range(HALVES):
-                nc.scalar.copy(out=h[b, t][:, u * BANK:(u + 1) * BANK], in_=acc[b, t, u][:])
+                nc.scalar.copy(out=h[j][:, u * BANK:(u + 1) * BANK], in_=acc[j, u][:])
 
-        def gather_x(b, t):
-            x[b, t] = keep.tile([P, M], F32, name="x%d%d" % (b, t), tag="x%d%d" % (b, t))
-            nc.vector.tensor_copy(x[b, t][:], h[b, t][:].indirect(pos1_sb[:]))
+        def gather_x(j):
+            x[j] = keep.tile([P, M], F32, name="x", tag="x%d" % j, align_bytes=64)
+            nc.vector.tensor_copy(x[j][:], h[j][:].indirect(pos1_sb[:]))
 
-        def silu_gain(b, t):
-            if t == 0:
-                zb[b] = keep.tile([P, PACK, M], BF16, name="zb%d" % b)
-            act = ring.tile([P, M], F32, name="act", tag="act", bufs=2)
-            nc.scalar.activation(act[:], x[b, t][:], ACT.Silu)
-            nc.scalar.activation(zb[b][:, t, :], act[:], ACT.Copy, scale=gain_sb[:, b, t:t + 1])
+        def silu_gain(j):
+            b, q = divmod(j, PACK)
+            act[j] = keep.tile([P, M], F32, name="act", tag="act%d" % (j % 2), align_bytes=64)
+            zb[j] = keep.tile([P, M], BF16, name="zb%d" % j)
+            nc.scalar.activation(act[j][:], x[j][:], ACT.Silu)
+            nc.scalar.activation(zb[j][:], act[j][:], ACT.Copy, scale=gain_sb[:, j:j + 1])
+            if q == 0:
+                zp[b] = keep.tile([P, PACK, M], BF16, name="zp", tag="raw%d2" % (2 - b), align_bytes=64)
+            for t in range(PACK):
+                nc.sync.dma_start(out=zp[b][q * QUAD:(q + 1) * QUAD, t, :], in_=zb[j][t:P:PACK, :])
 
-        def make_z(b):
-            zi[b] = keep.tile([P, M * PACK], BF16, name="zi%d" % b, tag="zi%d" % b, align_bytes=64)
+        def interleave_z(b):
+            zi[b] = keep.tile([P, M * PACK], BF16, name="zi", tag="zi%d" % b, align_bytes=64)
             nc.vector.tensor_copy(out=zi[b][:].rearrange("p (c i t) -> p c t i", i=4, t=PACK),
-                                  in_=zb[b][:].rearrange("p t (c i) -> p c t i", i=4))
-            quantize(("z", b, 0), zi[b])
+                                  in_=zp[b][:].rearrange("p t (c i) -> p c t i", i=4))
 
-        def gather_skip(b, t, dst):
-            nc.vector.tensor_copy(dst, h[b, t][:].indirect(pos2_sb[:]))
-            for q in range(P // QUAD):
-                n = PACK * b + q
-                if t == 0:
-                    skip[n] = keep.tile([P, M], F32, name="skip%d" % n)
-                nc.sync.dma_start(out=skip[n][t:P:PACK, :], in_=dst[q * QUAD:(q + 1) * QUAD, :])
+        def gather_skip(n, dst):
+            skip[n] = dst
+            nc.vector.tensor_copy(dst, h[n][:].indirect(pos2_sb[:]))
 
         def product_pass(a, n):
             if a == 0:
@@ -144,17 +151,17 @@ def tile_list_mural_retouch_advice_kernel(tc, tab_words, tab_scales, offs, pos1,
             nc.tensor.matmul_mx(
                 out=ya[n][:], lhsT=wa_w[:, a, 2 * n * P:2 * (n + 1) * P].bitcast(FP4X4),
                 lhsT_scale=wa_sc[:, a, n * P:(n + 1) * P],
-                rhs=codes[z][:].bitcast(FP8X4), rhs_scale=scales[z][:], start=(a == 0), stop=(a == R_PASSES - 1))
-            key, c = ("b", a, n // PACK), n % PACK
+                rhs=codes[z][:].bitcast(FP8X4), rhs_scale=scales[z], start=(a == 0), stop=(a == R_PASSES - 1))
+            key, c = ("b", a, n // 2), n % 2
             nc.tensor.matmul_mx(
                 out=yb[n][:], lhsT=codes[key][:, c * P:(c + 1) * P].bitcast(FP8X4),
                 lhsT_scale=scales[key][:, c * P:(c + 1) * P],
-                rhs=codes[z][:].bitcast(FP8X4), rhs_scale=scales[z][:], start=(a == 0), stop=(a == R_PASSES - 1))
+                rhs=codes[z][:].bitcast(FP8X4), rhs_scale=scales[z], start=(a == 0), stop=(a == R_PASSES - 1))
 
         def larger(n):
-            ya_sb = ring.tile([P, M], F32, name="ya_sb", tag="ya_sb", bufs=2)
+            ya_sb = ring.tile([P, M], F32, name="ya_sb", tag="ya_sb", bufs=3)
             nc.scalar.copy(out=ya_sb[:], in_=ya[n][:])
-            top[n] = ring.tile([P, M], F32, name="top", tag="top")
+            top[n] = ring.tile([P, M], F32, name="top", tag="top", bufs=2)
             nc.vector.tensor_tensor(top[n][:], yb[n][:], ya_sb[:], ALU.max)
 
         def finish(n, c0=0, c1=M):
@@ -164,107 +171,91 @@ def tile_list_mural_retouch_advice_kernel(tc, tab_words, tab_scales, offs, pos1,
 
         nc.vector.memset(tab_sc[:], 0)
         nc.vector.memset(wa_sc[:].bitcast(I32), 0)
-        warm = keep.tile([P, 8], F32, name="warm")
-        nc.gpsimd.memset(warm[:], 0.0)
-        nc.scalar.activation(warm[:], warm[:], ACT.Silu)
+        nc.vector.memset(rows[:], 0.0)
+        make_identity(nc, ident[:])
 
         nc.sync.dma_start(offs_sb[:], offs)
         load_tab(0)
-        load_w(w1, ("w", 0, 0), 0, KP)
+        load_w1(0, 0)
         for q in range(4):
             nc.sync.dma_start(out=tab_sc[QUAD * q:QUAD * q + 4 * K_PASSES, :],
                               in_=tab_scales[:, 4 * q:4 * q + 4, :].bitcast(I32))
         load_tab(1)
-        load_w(w1, ("w", 1, 0), 0, KP)
+        load_w1(1, 0)
         load_tab(2)
-        load_w(w1, ("w", 2, 0), 0, KP // 2, tag="half0")
-        load_w(w1, ("w", 2, 0), KP // 2, KP // 2, tag="half1")
+        load_w1(2, 0)
         nc.sync.dma_start(pos1_sb[:], pos1)
-        load_w(w1, ("w", 0, 1), KP, KP)
-        load_w(w1, ("w", 1, 1), KP, KP, tag="late1")
-        load_w(w1, ("w", 2, 1), KP, KP, tag="late2")
-        nc.sync.dma_start(pos2_sb[:], pos2)
-        nc.sync.dma_start(out=gain_sb[:], in_=gain.rearrange("(b p t) -> p b t", b=R_PASSES, t=PACK))
-
-        for u in range(HALVES):
-            gather_tab(0, u)
-        nc.vector.tensor_copy(v_sc[:], tab_sc[:].bitcast(U8).indirect(offs_sb[:]))
         for a in range(K_PASSES):
-            if a > 0:
-                for u in range(HALVES):
-                    gather_tab(a, u)
-            if a < K_PASSES - 1:
-                cast("scalar", ("w", a, 0))
-            else:
-                cast("scalar", ("w", a, 0), 0)
-                cast("vector", ("w", a, 0), 1)
-            quantize(("w", a, 0), grouped["w", a, 0])
-            for t in range(PACK):
-                for u in range(HALVES):
-                    encoder_pass(a, 0, t, u)
-
-        cast("vector", ("w", 0, 1))
-        quantize(("w", 0, 1), grouped["w", 0, 1])
-        load_w(wb, ("b", 0, 0), 0, KP)
+            load_w1(a, 1)
+        nc.sync.dma_start(out=rows[0:TILES, :], in_=gain.rearrange("(n p) -> n p", p=P))
+        nc.sync.dma_start(out=rows[TILES:2 * TILES, :], in_=sk.rearrange("(n p) -> n p", p=P))
+        nc.sync.dma_start(pos2_sb[:], pos2)
+        for a in range(K_PASSES):
+            load_w1(a, 2, 2)
+        for a in range(R_PASSES):
+            load_w(wb, "b", a, 0, GROUPS, "big%d" % a)
         nc.sync.dma_start(out=wa_w[:].bitcast(I32), in_=wa_words.bitcast(I32).rearrange("a p c -> p a c"))
         for q in range(4):
             nc.sync.dma_start(out=wa_sc[QUAD * q:QUAD * q + 4, :, :].bitcast(I32),
                               in_=wa_scales[:, 4 * q:4 * q + 4, :].bitcast(I32).rearrange("a r c -> r a c"))
-        load_w(wb, ("b", 1, 0), 0, KP)
-        load_w(wb, ("b", 0, 1), KP, KP)
-        load_w(wb, ("b", 1, 1), KP, KP)
-        with nc.allow_non_contiguous_dma(reason="one skip factor for each output row, one row to a partition"):
-            nc.sync.dma_start(out=sk_sb[:], in_=sk.rearrange("(n p) -> p n", p=P))
-        for t in range(PACK):
-            fetch_h(0, t)
-        for a in range(1, K_PASSES):
-            cast("scalar" if a == 1 else "scalar", ("w", a, 1))
-            quantize(("w", a, 1), grouped["w", a, 1])
-        for t in range(PACK):
-            for u in range(HALVES):
+
+        gather_tab(0, 1)
+        nc.vector.tensor_copy(v_sc[:], tab_sc[:].bitcast(U8).indirect(offs_sb[:]))
+        for a in range(K_PASSES):
+            if a > 0:
+                gather_tab(a, 1 if a < K_PASSES - 1 else HALVES)
+            weights(("w", a, 0), "scalar")
+            encoder(a, 0)
+
+        for g in range(GROUPS):
+            fetch_h(2 * g)
+            fetch_h(2 * g + 1)
+            if g + 1 < GROUPS:
                 for a in range(K_PASSES):
-                    encoder_pass(a, 1, t, u)
-        nc.vector.tensor_scalar(neg_sk[:], sk_sb[:], -1.0, None, ALU.mult)
-
-        def cast_wb(a, b):
-            for part in range(2):
-                cast("vector" if (a, b, part) in ((0, 0, 0), (0, 0, 1)) else "scalar", ("b", a, b), part)
-            quantize(("b", a, b), grouped["b", a, b])
-
-        for b in range(R_PASSES):
-            for t in range(PACK):
-                if b == 1:
-                    fetch_h(1, t)
-                gather_x(b, t)
-            for t in range(PACK):
-                silu_gain(b, t)
-            make_z(b)
-            if b == 0:
-                cast_wb(0, 0)
-                cast_wb(1, 0)
-        for pair in range(2):
-            held = keep.tile([P, 2, M], F32, name="held_late", tag="late%d" % (pair + 1))
-            for i in range(2):
-                gather_skip(0, 2 * pair + i, held[:, i, :])
-        for t in range(PACK):
-            if t < 3:
-                held = keep.tile([P, M], F32, name="held", tag="x1%d" % t)
-            else:
-                held = keep.tile([P, M], F32, name="held", tag="zi%d" % (t - 2), align_bytes=64)
-            gather_skip(1, t, held[:])
+                    weights(("w", a, g + 1), "scalar" if (a, g + 1) in ON_SCALAR else "vector")
+                    encoder(a, g + 1)
+            if g == 0:
+                turned = psum.tile([P, P], F32, name="turned", tag="bank")
+                nc.tensor.transpose(turned[:], rows[:], ident[:])
+                nc.scalar.copy(out=gain_sb[:], in_=turned[:, 0:TILES])
+                nc.scalar.activation(neg_sk[:], turned[:, TILES:2 * TILES], ACT.Copy, scale=-1.0)
+            gather_x(2 * g)
+            gather_x(2 * g + 1)
+            if g > 0:
+                silu_gain(2 * g - 2)
+                silu_gain(2 * g - 1)
+        silu_gain(TILES - 2)
+        silu_gain(TILES - 1)
+        interleave_z(0)
+        quantize(("z", 0, 0), zi[0], M)
+        for n in range(6):
+            held = keep.tile([P, M], F32, name="held", tag="x%d" % n, align_bytes=64)
+            gather_skip(n, held[:])
+        interleave_z(1)
+        wb_sc = keep.tile([P, R_PASSES * H], U8, name="wb_sc", tag="raw12", align_bytes=64)
+        for g in range(GROUPS):
+            for a in range(R_PASSES):
+                scales["b", a, g] = wb_sc[:, (R_PASSES * g + a) * GROUP:(R_PASSES * g + a + 1) * GROUP]
+        quantize(("z", 1, 0), zi[1], M)
+        for g in range(2):
+            for a in range(R_PASSES):
+                weights(("b", a, g), "scalar")
+            if g == 0:
+                late = keep.tile([P, 2, M], F32, name="late", tag="zi1", align_bytes=64)
+            gather_skip(6 + g, late[:, g, :])
 
         for a in range(R_PASSES):
             for n in range(PACK):
                 product_pass(a, n)
-        for n in range(OUT_TILES):
-            if n == 2:
-                cast_wb(0, 1)
-                cast_wb(1, 1)
+        for n in range(TILES):
+            if n in (1, 3):
+                for a in range(R_PASSES):
+                    weights(("b", a, 2 + n // 2), "scalar")
             if n >= PACK:
                 for a in range(R_PASSES):
                     product_pass(a, n)
             larger(n)
             if n > 0:
                 finish(n - 1)
-        finish(OUT_TILES - 1, 0, M // 2)
-        finish(OUT_TILES - 1, M // 2, M)
+        finish(TILES - 1, 0, M // 2)
+        finish(TILES - 1, M // 2, M)

@@ -28,7 +28,7 @@ HALVES = S // BANK
 TILES = H // P
 GROUP = 2 * P
 GROUPS = H // GROUP
-ON_SCALAR = ((0, 1), (0, 2))
+ON_SCALAR = ((0, 1), (0, 2), (1, 2), (1, 3), (2, 3))
 
 
 def tile_list_mural_retouch_advice_kernel(tc, tab_words, tab_scales, offs, pos1, pos2, w1, gain,

@@ -28,7 +28,7 @@ HALVES = S // BANK
 TILES = H // P
 GROUP = 2 * P
 GROUPS = H // GROUP
-ON_SCALAR = ((0, 1), (0, 2), (1, 2), (1, 3), (2, 3))
+ON_VECTOR = (("w", 1, 1), ("w", 2, 1), ("w", 1, 2), ("w", 1, 3), ("w", 2, 2))
 
 
 def tile_list_mural_retouch_advice_kernel(tc, tab_words, tab_scales, offs, pos1, pos2, w1, gain,
@@ -50,7 +50,7 @@ def tile_list_mural_retouch_advice_kernel(tc, tab_words, tab_scales, offs, pos1,
         wa_w = keep.tile([P, R_PASSES, 2 * H], U8, name="wa_w", align_bytes=64)
         wa_sc = keep.tile([P, R_PASSES, H], U8, name="wa_sc", align_bytes=64)
         v_sc = keep.tile([P, S], U8, name="v_sc", align_bytes=64)
-        tab_w, v_w, raw, grouped, codes, scales = {}, {}, {}, {}, {}, {}
+        tab_w, v_w, raw, codes, scales = {}, {}, {}, {}, {}
         acc, h, x, act, zb, zp, zi, skip, ya, yb, top = {}, {}, {}, {}, {}, {}, {}, {}, {}, {}, {}
 
         def load_tab(a):
@@ -67,28 +67,34 @@ def tile_list_mural_retouch_advice_kernel(tc, tab_words, tab_scales, offs, pos1,
         def load_w1(a, g, groups=1):
             load_w(w1, "w", a, g, groups, "raw%d%d" % (a, g))
 
-        def cast(engine, key):
-            if key[0] == "w":
-                grouped[key] = ring.tile([P, PACK * GROUP], BF16, name="grouped", tag="grouped", bufs=4, align_bytes=64)
-            else:
-                tag = ("x6", "act0", "x7", "act1")[(R_PASSES * key[2] + key[1]) % 4]
-                grouped[key] = keep.tile([P, PACK * GROUP], BF16, name="grouped_b", tag=tag, align_bytes=64)
-            dst = grouped[key][:].rearrange("p (m i j) -> p m j i", i=4, j=PACK)
+        def cast(engine, key, dst):
+            dst = dst.rearrange("p (m i j) -> p m j i", i=4, j=PACK)
             src = raw[key].rearrange("p j (m i) -> p m j i", i=4)
             if engine == "vector":
                 nc.vector.tensor_copy(out=dst, in_=src)
             else:
                 nc.scalar.copy(out=dst, in_=src)
 
-        def quantize(key, src, width):
-            codes[key] = keep.tile([P, width], U32, name="codes_%s%d%d" % key, align_bytes=64)
-            if key not in scales:
-                scales[key] = keep.tile([P, width], U8, name="scales_%s%d%d" % key, align_bytes=64)[:]
-            nc.vector.quantize_mx(out=codes[key][:].bitcast(FP8X4), scales=scales[key], in_=src[:])
+        def quantize(keys, src, width, plane=None):
+            n = len(keys) * width
+            words = keep.tile([P, n], U32, name="codes_%s%d%d" % keys[0], align_bytes=64)
+            if plane is None:
+                plane = keep.tile([P, n], U8, name="scales_%s%d%d" % keys[0], align_bytes=64)[:]
+            nc.vector.quantize_mx(out=words[:].bitcast(FP8X4), scales=plane, in_=src)
+            for e, key in enumerate(keys):
+                codes[key] = words[:, e * width:(e + 1) * width]
+                scales[key] = plane[:, e * width:(e + 1) * width]
 
-        def weights(key, engine):
-            cast(engine, key)
-            quantize(key, grouped[key], GROUP)
+        def weights(keys, plane=None):
+            unit = PACK * GROUP
+            if keys[0][0] == "w":
+                grouped = ring.tile([P, len(keys) * unit], BF16, name="grouped", tag="grouped", bufs=4, align_bytes=64)
+            else:
+                grouped = keep.tile([P, len(keys) * unit], BF16, name="grouped_b", tag="act%d" % (1 - keys[0][2] % 2),
+                                    align_bytes=64)
+            for e, key in enumerate(keys):
+                cast("vector" if key in ON_VECTOR else "scalar", key, grouped[:, e * unit:(e + 1) * unit])
+            quantize(keys, grouped[:], GROUP, plane)
 
         def gather_tab(a, pieces):
             v_w[a] = keep.tile([P, S], U32, name="v_w%d" % a, align_bytes=64)
@@ -120,7 +126,7 @@ def tile_list_mural_retouch_advice_kernel(tc, tab_words, tab_scales, offs, pos1,
                 nc.scalar.copy(out=h[j][:, u * BANK:(u + 1) * BANK], in_=acc[j, u][:])
 
         def gather_x(j):
-            x[j] = keep.tile([P, M], F32, name="x", tag="x%d" % j, align_bytes=64)
+            x[j] = keep.tile([P, M], F32, name="x", tag="raw%d%d" % (j % K_PASSES, j // K_PASSES) if j < 2 * K_PASSES else "x%d" % j, align_bytes=64)
             nc.vector.tensor_copy(x[j][:], h[j][:].indirect(pos1_sb[:]))
 
         def silu_gain(j):
@@ -130,9 +136,8 @@ def tile_list_mural_retouch_advice_kernel(tc, tab_words, tab_scales, offs, pos1,
             nc.scalar.activation(act[j][:], x[j][:], ACT.Silu)
             nc.scalar.activation(zb[j][:], act[j][:], ACT.Copy, scale=gain_sb[:, j:j + 1])
             if q == 0:
-                zp[b] = keep.tile([P, PACK, M], BF16, name="zp", tag="raw%d2" % (2 - b), align_bytes=64)
-            for t in range(PACK):
-                nc.sync.dma_start(out=zp[b][q * QUAD:(q + 1) * QUAD, t, :], in_=zb[j][t:P:PACK, :])
+                zp[b] = keep.tile([P, PACK, M], BF16, name="zp", tag="raw%d2" % b, align_bytes=64)
+            nc.sync.dma_start(out=zp[b][q * QUAD:(q + 1) * QUAD, :, :], in_=zb[j][:])
 
         def interleave_z(b):
             zi[b] = keep.tile([P, M * PACK], BF16, name="zi", tag="zi%d" % b, align_bytes=64)
@@ -143,7 +148,7 @@ def tile_list_mural_retouch_advice_kernel(tc, tab_words, tab_scales, offs, pos1,
             skip[n] = dst
             nc.vector.tensor_copy(dst, h[n][:].indirect(pos2_sb[:]))
 
-        def product_pass(a, n):
+        def pass_a(a, n):
             if a == 0:
                 ya[n] = psum.tile([P, M], F32, name="ya", tag="bank")
                 yb[n] = psum.tile([P, M], F32, name="yb", tag="bank")
@@ -151,12 +156,15 @@ def tile_list_mural_retouch_advice_kernel(tc, tab_words, tab_scales, offs, pos1,
             nc.tensor.matmul_mx(
                 out=ya[n][:], lhsT=wa_w[:, a, 2 * n * P:2 * (n + 1) * P].bitcast(FP4X4),
                 lhsT_scale=wa_sc[:, a, n * P:(n + 1) * P],
-                rhs=codes[z][:].bitcast(FP8X4), rhs_scale=scales[z], start=(a == 0), stop=(a == R_PASSES - 1))
+                rhs=codes[z].bitcast(FP8X4), rhs_scale=scales[z], start=(a == 0), stop=(a == R_PASSES - 1))
+
+        def pass_b(a, n):
+            z = ("z", a, 0)
             key, c = ("b", a, n // 2), n % 2
             nc.tensor.matmul_mx(
                 out=yb[n][:], lhsT=codes[key][:, c * P:(c + 1) * P].bitcast(FP8X4),
                 lhsT_scale=scales[key][:, c * P:(c + 1) * P],
-                rhs=codes[z][:].bitcast(FP8X4), rhs_scale=scales[z], start=(a == 0), stop=(a == R_PASSES - 1))
+                rhs=codes[z].bitcast(FP8X4), rhs_scale=scales[z], start=(a == 0), stop=(a == R_PASSES - 1))
 
         def larger(n):
             ya_sb = ring.tile([P, M], F32, name="ya_sb", tag="ya_sb", bufs=3)
@@ -169,6 +177,9 @@ def tile_list_mural_retouch_advice_kernel(tc, tab_words, tab_scales, offs, pos1,
                                            ALU.mult, ALU.add)
             nc.sync.dma_start(out=out[n * P:(n + 1) * P, c0:c1], in_=skip[n][:, c0:c1])
 
+        warm = keep.tile([P, 1], F32, name="warm")
+        nc.gpsimd.memset(warm[:], 0.0)
+        nc.scalar.activation(warm[:], warm[:], ACT.Silu)
         nc.vector.memset(tab_sc[:], 0)
         nc.vector.memset(wa_sc[:].bitcast(I32), 0)
         nc.vector.memset(rows[:], 0.0)
@@ -201,59 +212,74 @@ def tile_list_mural_retouch_advice_kernel(tc, tab_words, tab_scales, offs, pos1,
 
         gather_tab(0, 1)
         nc.vector.tensor_copy(v_sc[:], tab_sc[:].bitcast(U8).indirect(offs_sb[:]))
-        for a in range(K_PASSES):
-            if a > 0:
-                gather_tab(a, 1 if a < K_PASSES - 1 else HALVES)
-            weights(("w", a, 0), "scalar")
-            encoder(a, 0)
+        weights([("w", 0, 0)])
+        encoder(0, 0)
+        gather_tab(1, 1)
+        weights([("w", 1, 0)])
+        encoder(1, 0)
+        gather_tab(2, HALVES)
+        weights([("w", 2, 0)])
+        encoder(2, 0)
 
-        for g in range(GROUPS):
-            fetch_h(2 * g)
-            fetch_h(2 * g + 1)
-            if g + 1 < GROUPS:
-                for a in range(K_PASSES):
-                    weights(("w", a, g + 1), "scalar" if (a, g + 1) in ON_SCALAR else "vector")
-                    encoder(a, g + 1)
-            if g == 0:
-                turned = psum.tile([P, P], F32, name="turned", tag="bank")
-                nc.tensor.transpose(turned[:], rows[:], ident[:])
-                nc.scalar.copy(out=gain_sb[:], in_=turned[:, 0:TILES])
-                nc.scalar.activation(neg_sk[:], turned[:, TILES:2 * TILES], ACT.Copy, scale=-1.0)
-            gather_x(2 * g)
-            gather_x(2 * g + 1)
-            if g > 0:
-                silu_gain(2 * g - 2)
-                silu_gain(2 * g - 1)
-        silu_gain(TILES - 2)
+        fetch_h(0)
+        fetch_h(1)
+        for a in range(K_PASSES):
+            weights([("w", a, 1)])
+            encoder(a, 1)
+        turned = psum.tile([P, P], F32, name="turned", tag="bank")
+        nc.tensor.transpose(turned[:], rows[:], ident[:])
+        nc.scalar.copy(out=gain_sb[:], in_=turned[:, 0:TILES])
+        nc.scalar.activation(neg_sk[:], turned[:, TILES:2 * TILES], ACT.Copy, scale=-1.0)
+        weights([("w", 0, 2)])
+        weights([("w", 0, 3)])
+        fetch_h(2)
+        fetch_h(3)
+        for a in range(1, K_PASSES):
+            weights([("w", a, 2)])
+            weights([("w", a, 3)])
+        for g in (2, 3):
+            for a in range(K_PASSES):
+                encoder(a, g)
+        for j in range(TILES):
+            if j >= PACK:
+                fetch_h(j)
+            gather_x(j)
+        for j in range(TILES - 1):
+            silu_gain(j)
         silu_gain(TILES - 1)
         interleave_z(0)
-        quantize(("z", 0, 0), zi[0], M)
-        for n in range(6):
-            held = keep.tile([P, M], F32, name="held", tag="x%d" % n, align_bytes=64)
-            gather_skip(n, held[:])
+        quantize([("z", 0, 0)], zi[0][:], M)
+        for first, count, tag in ((0, 2, "raw22"), (2, 2, "raw01"), (4, 3, "raw11")):
+            held = keep.tile([P, count, M], F32, name="held", tag=tag, align_bytes=64)
+            for n in range(count):
+                gather_skip(first + n, held[:, n, :])
         interleave_z(1)
         wb_sc = keep.tile([P, R_PASSES * H], U8, name="wb_sc", tag="raw12", align_bytes=64)
-        for g in range(GROUPS):
-            for a in range(R_PASSES):
-                scales["b", a, g] = wb_sc[:, (R_PASSES * g + a) * GROUP:(R_PASSES * g + a + 1) * GROUP]
-        quantize(("z", 1, 0), zi[1], M)
-        for g in range(2):
-            for a in range(R_PASSES):
-                weights(("b", a, g), "scalar")
-            if g == 0:
-                late = keep.tile([P, 2, M], F32, name="late", tag="zi1", align_bytes=64)
-            gather_skip(6 + g, late[:, g, :])
 
-        for a in range(R_PASSES):
-            for n in range(PACK):
-                product_pass(a, n)
+        def weights_b(g):
+            weights([("b", a, g) for a in range(R_PASSES)], wb_sc[:, g * KP:(g + 1) * KP])
+
+        quantize([("z", 1, 0)], zi[1][:], M)
+        for g in range(2):
+            weights_b(g)
+            if g == 0:
+                late = keep.tile([P, M], F32, name="late", tag="zi1", align_bytes=64)
+                gather_skip(TILES - 1, late[:])
+
+        for n in range(PACK):
+            pass_a(0, n)
+        for n in range(PACK):
+            pass_a(1, n)
+            pass_b(0, n)
+            pass_b(1, n)
         for n in range(TILES):
             if n in (1, 3):
-                for a in range(R_PASSES):
-                    weights(("b", a, 2 + n // 2), "scalar")
+                weights_b(2 + n // 2)
             if n >= PACK:
                 for a in range(R_PASSES):
-                    product_pass(a, n)
+                    pass_a(a, n)
+                for a in range(R_PASSES):
+                    pass_b(a, n)
             larger(n)
             if n > 0:
                 finish(n - 1)

@@ -177,9 +177,6 @@ def tile_list_mural_retouch_advice_kernel(tc, tab_words, tab_scales, offs, pos1,
                                            ALU.mult, ALU.add)
             nc.sync.dma_start(out=out[n * P:(n + 1) * P, c0:c1], in_=skip[n][:, c0:c1])
 
-        warm = keep.tile([P, 1], F32, name="warm")
-        nc.gpsimd.memset(warm[:], 0.0)
-        nc.scalar.activation(warm[:], warm[:], ACT.Silu)
         nc.vector.memset(tab_sc[:], 0)
         nc.vector.memset(wa_sc[:].bitcast(I32), 0)
         nc.vector.memset(rows[:], 0.0)

@@ -198,8 +198,10 @@ def tile_list_mural_retouch_advice_kernel(tc, tab_words, tab_scales, offs, pos1,
         nc.sync.dma_start(out=rows[0:TILES, :], in_=gain.rearrange("(n p) -> n p", p=P))
         nc.sync.dma_start(out=rows[TILES:2 * TILES, :], in_=sk.rearrange("(n p) -> n p", p=P))
         nc.sync.dma_start(pos2_sb[:], pos2)
-        for a in range(K_PASSES):
+        for a in range(K_PASSES - 1):
             load_w1(a, 2, 2)
+        for g in (2, 3):
+            load_w1(K_PASSES - 1, g)
         for a in range(R_PASSES):
             load_w(wb, "b", a, 0, GROUPS, "big%d" % a)
         nc.sync.dma_start(out=wa_w[:].bitcast(I32), in_=wa_words.bitcast(I32).rearrange("a p c -> p a c"))
@@ -246,7 +248,7 @@ def tile_list_mural_retouch_advice_kernel(tc, tab_words, tab_scales, offs, pos1,
         silu_gain(TILES - 1)
         interleave_z(0)
         quantize([("z", 0, 0)], zi[0][:], M)
-        for first, count, tag in ((0, 2, "raw22"), (2, 2, "raw01"), (4, 3, "raw11")):
+        for first, count, tag in ((0, 2, "raw23"), (2, 2, "raw01"), (4, 3, "raw11")):
             held = keep.tile([P, count, M], F32, name="held", tag=tag, align_bytes=64)
             for n in range(count):
                 gather_skip(first + n, held[:, n, :])

@@ -28,7 +28,7 @@ HALVES = S // BANK
 TILES = H // P
 GROUP = 2 * P
 GROUPS = H // GROUP
-ON_VECTOR = (("w", 1, 1), ("w", 2, 1), ("w", 1, 2), ("w", 1, 3), ("w", 2, 2))
+ON_VECTOR = (("w", 1, 1), ("w", 2, 1), ("w", 1, 2), ("w", 2, 2))
 
 
 def tile_list_mural_retouch_advice_kernel(tc, tab_words, tab_scales, offs, pos1, pos2, w1, gain,
@@ -198,10 +198,10 @@ def tile_list_mural_retouch_advice_kernel(tc, tab_words, tab_scales, offs, pos1,
         nc.sync.dma_start(out=rows[0:TILES, :], in_=gain.rearrange("(n p) -> n p", p=P))
         nc.sync.dma_start(out=rows[TILES:2 * TILES, :], in_=sk.rearrange("(n p) -> n p", p=P))
         nc.sync.dma_start(pos2_sb[:], pos2)
-        for a in range(K_PASSES - 1):
-            load_w1(a, 2, 2)
+        load_w1(0, 2, 2)
         for g in (2, 3):
-            load_w1(K_PASSES - 1, g)
+            for a in range(1, K_PASSES):
+                load_w1(a, g)
         for a in range(R_PASSES):
             load_w(wb, "b", a, 0, GROUPS, "big%d" % a)
         nc.sync.dma_start(out=wa_w[:].bitcast(I32), in_=wa_words.bitcast(I32).rearrange("a p c -> p a c"))
@@ -233,9 +233,9 @@ def tile_list_mural_retouch_advice_kernel(tc, tab_words, tab_scales, offs, pos1,
         weights([("w", 0, 3)])
         fetch_h(2)
         fetch_h(3)
-        for a in range(1, K_PASSES):
-            weights([("w", a, 2)])
-            weights([("w", a, 3)])
+        for g in (2, 3):
+            for a in range(1, K_PASSES):
+                weights([("w", a, g)])
         for g in (2, 3):
             for a in range(K_PASSES):
                 encoder(a, g)

@@ -68,10 +68,14 @@ def tile_list_mural_retouch_advice_kernel(tc, tab_words, tab_scales, offs, pos1,
             load_w(w1, "w", a, g, groups, "raw%d%d" % (a, g))
 
         def cast(engine, key, dst):
+            flat = dst
             dst = dst.rearrange("p (m i j) -> p m j i", i=4, j=PACK)
             src = raw[key].rearrange("p j (m i) -> p m j i", i=4)
             if engine == "vector":
                 nc.vector.tensor_copy(out=dst, in_=src)
+            elif engine == "gpsimd":
+                nc.gpsimd.tensor_scalar(flat.rearrange("p (c j) -> p c j", j=PACK), raw[key].rearrange("p j c -> p c j"),
+                                        1.0, 0.0, ALU.mult, ALU.add)
             else:
                 nc.scalar.copy(out=dst, in_=src)
 
@@ -90,10 +94,10 @@ def tile_list_mural_retouch_advice_kernel(tc, tab_words, tab_scales, offs, pos1,
             if keys[0][0] == "w":
                 grouped = ring.tile([P, len(keys) * unit], BF16, name="grouped", tag="grouped", bufs=4, align_bytes=64)
             else:
-                grouped = keep.tile([P, len(keys) * unit], BF16, name="grouped_b", tag="act%d" % (1 - keys[0][2] % 2),
+                grouped = keep.tile([P, len(keys) * unit], BF16, name="grouped_b", tag=("act1", "act0", "late2", "late3")[keys[0][2]],
                                     align_bytes=64)
             for e, key in enumerate(keys):
-                cast("vector" if key in ON_VECTOR else "scalar", key, grouped[:, e * unit:(e + 1) * unit])
+                cast("vector" if key in ON_VECTOR else "gpsimd" if key[0] == "b" and key[2] >= 2 else "scalar", key, grouped[:, e * unit:(e + 1) * unit])
             quantize(keys, grouped[:], GROUP, plane)
 
         def gather_tab(a, pieces):

@@ -89,16 +89,10 @@ def tile_list_mural_retouch_advice_kernel(tc, tab_words, tab_scales, offs, pos1,
                 codes[key] = words[:, e * width:(e + 1) * width]
                 scales[key] = plane[:, e * width:(e + 1) * width]
 
-        def weights(keys, plane=None):
-            unit = PACK * GROUP
-            if keys[0][0] == "w":
-                grouped = ring.tile([P, len(keys) * unit], BF16, name="grouped", tag="grouped", bufs=4, align_bytes=64)
-            else:
-                grouped = keep.tile([P, len(keys) * unit], BF16, name="grouped_b", tag=("act1", "act0", "late2", "late3")[keys[0][2]],
-                                    align_bytes=64)
-            for e, key in enumerate(keys):
-                cast("vector" if key in ON_VECTOR else "gpsimd" if key[0] == "b" and key[2] >= 2 else "scalar", key, grouped[:, e * unit:(e + 1) * unit])
-            quantize(keys, grouped[:], GROUP, plane)
+        def weights(keys):
+            grouped = ring.tile([P, PACK * GROUP], BF16, name="grouped", tag="grouped", bufs=4, align_bytes=64)
+            cast("vector" if keys[0] in ON_VECTOR else "scalar", keys[0], grouped[:])
+            quantize(keys, grouped[:], GROUP)
 
         def gather_tab(a, pieces):
             v_w[a] = keep.tile([P, S], U32, name="v_w%d" % a, align_bytes=64)
@@ -145,7 +139,8 @@ def tile_list_mural_retouch_advice_kernel(tc, tab_words, tab_scales, offs, pos1,
 
         def interleave_z(b):
             zi[b] = keep.tile([P, M * PACK], BF16, name="zi", tag="zi%d" % b, align_bytes=64)
-            nc.vector.tensor_copy(out=zi[b][:].rearrange("p (c i t) -> p c t i", i=4, t=PACK),
+            copy = (nc.vector.tensor_copy, nc.scalar.copy)[b]
+            copy(out=zi[b][:].rearrange("p (c i t) -> p c t i", i=4, t=PACK),
                                   in_=zp[b][:].rearrange("p t (c i) -> p c t i", i=4))
 
         def gather_skip(n, dst):
@@ -256,11 +251,27 @@ def tile_list_mural_retouch_advice_kernel(tc, tab_words, tab_scales, offs, pos1,
             held = keep.tile([P, count, M], F32, name="held", tag=tag, align_bytes=64)
             for n in range(count):
                 gather_skip(first + n, held[:, n, :])
+        unit = PACK * GROUP
+        rounded = {}
+        for g in range(GROUPS):
+            both = keep.tile([P, unit * (1 if g < 2 else 2)], BF16, name="rounded%d" % g, align_bytes=64)
+            rounded[0, g] = both[:, 0:unit]
+            rounded["both", g] = both[:]
+            cast("gpsimd", ("b", 0, g), rounded[0, g])
+        for g in (2, 3):
+            cast("gpsimd", ("b", 1, g), rounded["both", g][:, unit:2 * unit])
+        for g in range(2):
+            rounded[1, g] = keep.tile([P, unit], BF16, name="rounded", tag="act%d" % (1 - g), align_bytes=64)[:]
+            cast("scalar", ("b", 1, g), rounded[1, g])
         interleave_z(1)
-        wb_sc = keep.tile([P, R_PASSES * H], U8, name="wb_sc", tag="raw12", align_bytes=64)
+        wb_sc = keep.tile([P, R_PASSES * H], U8, name="wb_sc", tag="raw02", align_bytes=64)
 
         def weights_b(g):
-            weights([("b", a, g) for a in range(R_PASSES)], wb_sc[:, g * KP:(g + 1) * KP])
+            if g < 2:
+                for a in range(R_PASSES):
+                    quantize([("b", a, g)], rounded[a, g], GROUP, wb_sc[:, g * KP + a * GROUP:g * KP + (a + 1) * GROUP])
+            else:
+                quantize([("b", a, g) for a in range(R_PASSES)], rounded["both", g], GROUP, wb_sc[:, g * KP:(g + 1) * KP])
 
         quantize([("z", 1, 0)], zi[1][:], M)
         for g in range(2):

@@ -254,20 +254,20 @@ def tile_list_mural_retouch_advice_kernel(tc, tab_words, tab_scales, offs, pos1,
         unit = PACK * GROUP
         rounded = {}
         for g in range(GROUPS):
-            both = keep.tile([P, unit * (1 if g < 2 else 2)], BF16, name="rounded%d" % g, align_bytes=64)
+            both = keep.tile([P, unit * (1 if g < 1 else 2)], BF16, name="rounded%d" % g, align_bytes=64)
             rounded[0, g] = both[:, 0:unit]
             rounded["both", g] = both[:]
             cast("gpsimd", ("b", 0, g), rounded[0, g])
-        for g in (2, 3):
+        for g in (1, 2, 3):
             cast("gpsimd", ("b", 1, g), rounded["both", g][:, unit:2 * unit])
-        for g in range(2):
+        for g in range(1):
             rounded[1, g] = keep.tile([P, unit], BF16, name="rounded", tag="act%d" % (1 - g), align_bytes=64)[:]
             cast("scalar", ("b", 1, g), rounded[1, g])
         interleave_z(1)
         wb_sc = keep.tile([P, R_PASSES * H], U8, name="wb_sc", tag="raw02", align_bytes=64)
 
         def weights_b(g):
-            if g < 2:
+            if g < 1:
                 for a in range(R_PASSES):
                     quantize([("b", a, g)], rounded[a, g], GROUP, wb_sc[:, g * KP + a * GROUP:g * KP + (a + 1) * GROUP])
             else:

@@ -28,7 +28,7 @@ HALVES = S // BANK
 TILES = H // P
 GROUP = 2 * P
 GROUPS = H // GROUP
-ON_VECTOR = (("w", 1, 1), ("w", 2, 1), ("w", 1, 2), ("w", 2, 2))
+UNIT = PACK * GROUP
 
 
 def tile_list_mural_retouch_advice_kernel(tc, tab_words, tab_scales, offs, pos1, pos2, w1, gain,
@@ -39,63 +39,69 @@ def tile_list_mural_retouch_advice_kernel(tc, tab_words, tab_scales, offs, pos1,
         ring = ctx.enter_context(tc.tile_pool(name="ring", bufs=3))
         psum = ctx.enter_context(tc.psum_pool(name="psum", bufs=8))
 
+        def held(name, shape, dtype, tag=None):
+            return keep.tile(shape, dtype, name=name, tag=tag or name, align_bytes=64)
+
         offs_sb = keep.tile([P, S // 16], U16, name="offs_sb")
         pos1_sb = keep.tile([P, M // 16], U16, name="pos1_sb")
         pos2_sb = keep.tile([P, M // 16], U16, name="pos2_sb")
-        rows = keep.tile([P, P], F32, name="rows")
-        ident = keep.tile([P, P], F32, name="ident")
-        gain_sb = keep.tile([P, TILES], F32, name="gain_sb")
-        neg_sk = keep.tile([P, TILES], F32, name="neg_sk")
-        tab_sc = keep.tile([P, T // 4], I32, name="tab_sc")
-        wa_w = keep.tile([P, R_PASSES, 2 * H], U8, name="wa_w", align_bytes=64)
-        wa_sc = keep.tile([P, R_PASSES, H], U8, name="wa_sc", align_bytes=64)
-        v_sc = keep.tile([P, S], U8, name="v_sc", align_bytes=64)
+        rows = held("rows", [P, P], F32)
+        ident = held("ident", [P, P], F32)
+        gain_sb = held("gain_sb", [P, TILES], F32)
+        neg_sk = held("neg_sk", [P, TILES], F32)
+        tab_sc = held("tab_sc", [P, T // 4], I32)
+        wa_sc = held("wa_sc", [P, R_PASSES, H], U8)
+        v_sc = held("v_sc", [P, S], U8)
         tab_w, v_w, raw, codes, scales = {}, {}, {}, {}, {}
-        acc, h, x, act, zb, zp, zi, skip, ya, yb, top = {}, {}, {}, {}, {}, {}, {}, {}, {}, {}, {}
+        acc, h, x, zb, zp, zi, skip, ya, yb, top = {}, {}, {}, {}, {}, {}, {}, {}, {}, {}
 
         def load_tab(a):
-            tab_w[a] = keep.tile([P, T], I32, name="tab_w%d" % a, tag="big%d" % a, align_bytes=64)
+            tab_w[a] = held("tab_w%d" % a, [P, T], I32, "big%d" % a)
             nc.sync.dma_start(out=tab_w[a][:], in_=tab_words[a].rearrange("p t i -> p (t i)").bitcast(I32))
 
         def load_w(w, name, a, g, groups, tag):
-            tile = keep.tile([P, PACK, groups * GROUP], F32, name="raw", tag=tag, align_bytes=64)
+            tile = held("raw", [P, PACK, groups * GROUP], F32, tag)
             nc.sync.dma_start(out=tile[:], in_=w[a * KP:(a + 1) * KP, g * GROUP:(g + groups) * GROUP]
                               .rearrange("(p j) c -> p j c", j=PACK))
             for e in range(groups):
                 raw[name, a, g + e] = tile[:, :, e * GROUP:(e + 1) * GROUP]
 
-        def load_w1(a, g, groups=1):
-            load_w(w1, "w", a, g, groups, "raw%d%d" % (a, g))
+        def load_w1(a, g):
+            load_w(w1, "w", a, g, 1, "raw%d%d" % (a, g))
 
         def cast(engine, key, dst):
-            flat = dst
-            dst = dst.rearrange("p (m i j) -> p m j i", i=4, j=PACK)
-            src = raw[key].rearrange("p j (m i) -> p m j i", i=4)
-            if engine == "vector":
-                nc.vector.tensor_copy(out=dst, in_=src)
-            elif engine == "gpsimd":
-                nc.gpsimd.tensor_scalar(flat.rearrange("p (c j) -> p c j", j=PACK), raw[key].rearrange("p j c -> p c j"),
+            if engine == "gpsimd":
+                nc.gpsimd.tensor_scalar(dst.rearrange("p (c j) -> p c j", j=PACK), raw[key].rearrange("p j c -> p c j"),
                                         1.0, 0.0, ALU.mult, ALU.add)
             else:
-                nc.scalar.copy(out=dst, in_=src)
+                copy = nc.vector.tensor_copy if engine == "vector" else nc.scalar.copy
+                copy(out=dst.rearrange("p (m i j) -> p m j i", i=4, j=PACK),
+                     in_=raw[key].rearrange("p j (m i) -> p m j i", i=4))
 
-        def quantize(keys, src, width, plane=None):
+        def quantize(keys, src, width, tag=None):
             n = len(keys) * width
-            words = keep.tile([P, n], U32, name="codes_%s%d%d" % keys[0], align_bytes=64)
-            if plane is None:
-                plane = keep.tile([P, n], U8, name="scales_%s%d%d" % keys[0], align_bytes=64)[:]
-            nc.vector.quantize_mx(out=words[:].bitcast(FP8X4), scales=plane, in_=src)
+            words = held("codes_%s%d%d" % keys[0], [P, n], U32, tag)
+            plane = held("scales_%s%d%d" % keys[0], [P, n], U8)
+            nc.vector.quantize_mx(out=words[:].bitcast(FP8X4), scales=plane[:], in_=src)
             for e, key in enumerate(keys):
                 codes[key] = words[:, e * width:(e + 1) * width]
                 scales[key] = plane[:, e * width:(e + 1) * width]
 
-        def weights(keys):
-            grouped = ring.tile([P, PACK * GROUP], BF16, name="grouped", tag="grouped", bufs=4, align_bytes=64)
-            cast("vector" if keys[0] in ON_VECTOR else "scalar", keys[0], grouped[:])
-            quantize(keys, grouped[:], GROUP)
+        def rounded(jobs, dst):
+            for e, (engine, key) in enumerate(jobs):
+                cast(engine, key, dst[:, e * UNIT:(e + 1) * UNIT])
+            return [key for engine, key in jobs]
+
+        def early_unit(engine, a, g):
+            grouped = ring.tile([P, UNIT], BF16, name="grouped", tag="grouped", align_bytes=64)
+            quantize(rounded([(engine, ("w", a, g))], grouped), grouped[:], GROUP)
+
+        def late_units(*jobs):
+            pair = held("pair", [P, len(jobs) * UNIT], BF16)
+            quantize(rounded([(engine, ("w", a, g)) for engine, a, g in jobs], pair), pair[:], GROUP)
 
         def gather_tab(a, pieces):
-            v_w[a] = keep.tile([P, S], U32, name="v_w%d" % a, align_bytes=64)
+            v_w[a] = held("v_w%d" % a, [P, S], U32)
             n = S // pieces
             for u in range(pieces):
                 nc.vector.tensor_copy(v_w[a][:, u * n:(u + 1) * n],
@@ -113,39 +119,46 @@ def tile_list_mural_retouch_advice_kernel(tc, tab_words, tab_scales, offs, pos1,
                 rhs_scale=v_sc[4 * a:P, u * BANK:(u + 1) * BANK],
                 start=(a == 0), stop=(a == K_PASSES - 1))
 
-        def encoder(a, g):
+        def encoder(passes, g):
             for j in (2 * g, 2 * g + 1):
                 for u in range(HALVES):
-                    encoder_pass(a, j, u)
+                    for a in passes:
+                        encoder_pass(a, j, u)
 
-        def fetch_h(j):
-            h[j] = keep.tile([P, S], F32, name="h%d" % j)
-            for u in range(HALVES):
-                nc.scalar.copy(out=h[j][:, u * BANK:(u + 1) * BANK], in_=acc[j, u][:])
+        def fetch_h(g):
+            for j in (2 * g, 2 * g + 1):
+                h[j] = held("h%d" % j, [P, S], F32)
+                for u in range(HALVES):
+                    nc.scalar.copy(out=h[j][:, u * BANK:(u + 1) * BANK], in_=acc[j, u][:])
 
-        def gather_x(j):
-            x[j] = keep.tile([P, M], F32, name="x", tag="raw%d%d" % (j % K_PASSES, j // K_PASSES) if j < 2 * K_PASSES else "x%d" % j, align_bytes=64)
-            nc.vector.tensor_copy(x[j][:], h[j][:].indirect(pos1_sb[:]))
+        def gathers(tag, *jobs, spare=0):
+            dst = held("picked", [P, len(jobs) + spare, M], F32, tag)
+            for e, (kind, j) in enumerate(jobs):
+                picked, places = (x, pos1_sb) if kind == "x" else (skip, pos2_sb)
+                picked[j] = dst[:, e, :]
+                nc.vector.tensor_copy(picked[j], h[j][:].indirect(places[:]))
+            return [dst[:, e, :] for e in range(len(jobs), len(jobs) + spare)]
 
-        def silu_gain(j):
+        def act_in(tag):
+            return held("act", [P, M], F32, tag)[:]
+
+        def silu_gain(j, act):
             b, q = divmod(j, PACK)
-            act[j] = keep.tile([P, M], F32, name="act", tag="act%d" % (j % 2), align_bytes=64)
-            zb[j] = keep.tile([P, M], BF16, name="zb%d" % j)
-            nc.scalar.activation(act[j][:], x[j][:], ACT.Silu)
-            nc.scalar.activation(zb[j][:], act[j][:], ACT.Copy, scale=gain_sb[:, j:j + 1])
             if q == 0:
-                zp[b] = keep.tile([P, PACK, M], BF16, name="zp", tag="raw%d2" % b, align_bytes=64)
-            nc.sync.dma_start(out=zp[b][q * QUAD:(q + 1) * QUAD, :, :], in_=zb[j][:])
+                zb[b] = held("zb%d" % b, [P, PACK, M], BF16, ("big1", None)[b])
+                zp[b] = held("zp", [P, PACK, M], BF16, "raw%d1" % b)
+            nc.scalar.activation(act, x[j], ACT.Silu)
+            nc.scalar.activation(zb[b][:, q, :], act, ACT.Copy, scale=gain_sb[:, j:j + 1])
+            nc.sync.dma_start(out=zp[b][q * QUAD:(q + 1) * QUAD, :, :], in_=zb[b][:, q, :])
 
-        def interleave_z(b):
-            zi[b] = keep.tile([P, M * PACK], BF16, name="zi", tag="zi%d" % b, align_bytes=64)
-            copy = (nc.vector.tensor_copy, nc.scalar.copy)[b]
-            copy(out=zi[b][:].rearrange("p (c i t) -> p c t i", i=4, t=PACK),
-                                  in_=zp[b][:].rearrange("p t (c i) -> p c t i", i=4))
-
-        def gather_skip(n, dst):
-            skip[n] = dst
-            nc.vector.tensor_copy(dst, h[n][:].indirect(pos2_sb[:]))
+        def interleave_z(engine, b, tag):
+            zi[b] = held("zi", [P, M * PACK], BF16, tag)
+            if engine == "gpsimd":
+                nc.gpsimd.tensor_scalar(zi[b][:].rearrange("p (c t) -> p c t", t=PACK), zp[b][:].rearrange("p t c -> p c t"),
+                                        1.0, 0.0, ALU.mult, ALU.add)
+            else:
+                nc.scalar.copy(out=zi[b][:].rearrange("p (c i t) -> p c t i", i=4, t=PACK),
+                               in_=zp[b][:].rearrange("p t (c i) -> p c t i", i=4))
 
         def pass_a(a, n):
             if a == 0:
@@ -197,98 +210,89 @@ def tile_list_mural_retouch_advice_kernel(tc, tab_words, tab_scales, offs, pos1,
         nc.sync.dma_start(out=rows[0:TILES, :], in_=gain.rearrange("(n p) -> n p", p=P))
         nc.sync.dma_start(out=rows[TILES:2 * TILES, :], in_=sk.rearrange("(n p) -> n p", p=P))
         nc.sync.dma_start(pos2_sb[:], pos2)
-        load_w1(0, 2, 2)
         for g in (2, 3):
-            for a in range(1, K_PASSES):
+            for a in range(K_PASSES):
                 load_w1(a, g)
-        for a in range(R_PASSES):
-            load_w(wb, "b", a, 0, GROUPS, "big%d" % a)
-        nc.sync.dma_start(out=wa_w[:].bitcast(I32), in_=wa_words.bitcast(I32).rearrange("a p c -> p a c"))
+        load_w(wb, "b", 0, 0, 2, "big0")
+        load_w(wb, "b", 1, 0, 2, "wb10")
         for q in range(4):
             nc.sync.dma_start(out=wa_sc[QUAD * q:QUAD * q + 4, :, :].bitcast(I32),
                               in_=wa_scales[:, 4 * q:4 * q + 4, :].bitcast(I32).rearrange("a r c -> r a c"))
 
         gather_tab(0, 1)
         nc.vector.tensor_copy(v_sc[:], tab_sc[:].bitcast(U8).indirect(offs_sb[:]))
-        weights([("w", 0, 0)])
-        encoder(0, 0)
+        early_unit("scalar", 0, 0)
+        encoder([0], 0)
         gather_tab(1, 1)
-        weights([("w", 1, 0)])
-        encoder(1, 0)
+        early_unit("scalar", 1, 0)
+        encoder([1], 0)
         gather_tab(2, HALVES)
-        weights([("w", 2, 0)])
-        encoder(2, 0)
-
+        early_unit("scalar", 2, 0)
+        encoder([2], 0)
         fetch_h(0)
-        fetch_h(1)
-        for a in range(K_PASSES):
-            weights([("w", a, 1)])
-            encoder(a, 1)
+        for a in (0, 1):
+            early_unit("vector", a, 1)
+            encoder([a], 1)
+        gathers("raw00", ("x", 0))
+        gathers("raw10", ("x", 1))
+        late_units(("scalar", 2, 1))
+        encoder([2], 1)
+        first_acts = gathers("raw21", ("s", 0), ("s", 1), spare=2)
         turned = psum.tile([P, P], F32, name="turned", tag="bank")
         nc.tensor.transpose(turned[:], rows[:], ident[:])
         nc.scalar.copy(out=gain_sb[:], in_=turned[:, 0:TILES])
         nc.scalar.activation(neg_sk[:], turned[:, TILES:2 * TILES], ACT.Copy, scale=-1.0)
-        weights([("w", 0, 2)])
-        weights([("w", 0, 3)])
+        fetch_h(1)
+        late_units(("gpsimd", 0, 2), ("gpsimd", 1, 2))
+        encoder([0, 1], 2)
+        gathers("raw12", ("x", 2), ("x", 3))
+        late_units(("gpsimd", 2, 2), ("gpsimd", 0, 3))
+        encoder([2], 2)
+        encoder([0], 3)
+        gathers("raw03", ("s", 2))
+        late_units(("gpsimd", 1, 3), ("scalar", 2, 3))
+        encoder([1, 2], 3)
         fetch_h(2)
         fetch_h(3)
-        for g in (2, 3):
-            for a in range(1, K_PASSES):
-                weights([("w", a, g)])
-        for g in (2, 3):
-            for a in range(K_PASSES):
-                encoder(a, g)
-        for j in range(TILES):
-            if j >= PACK:
-                fetch_h(j)
-            gather_x(j)
-        for j in range(TILES - 1):
-            silu_gain(j)
-        silu_gain(TILES - 1)
-        interleave_z(0)
+        gathers("raw23", ("x", 4), ("x", 5), ("s", 3))
+        gathers("raw02", ("x", 6), ("x", 7))
+        silu_gain(0, first_acts[0])
+        silu_gain(1, first_acts[1])
+        silu_gain(2, act_in("wa_w"))
+        wa_w = held("wa_w", [P, R_PASSES, 2 * H], U8)
+        nc.sync.dma_start(out=wa_w[:].bitcast(I32), in_=wa_words.bitcast(I32).rearrange("a p c -> p a c"))
+        silu_gain(3, act_in("big2"))
+        load_w(wb, "b", 0, 2, 2, "big2")
+        load_w(wb, "b", 1, 2, 2, "big1")
+        for j, tag in zip(range(PACK, TILES), ("act0", "raw22", "act0", "act1")):
+            silu_gain(j, act_in(tag))
+        gathers("raw22", ("s", 4), ("s", 5))
+        gathers("raw02", ("s", 6))
+
+        first = held("first", [P, 4 * UNIT], BF16)
+        first_keys = rounded([("gpsimd", ("b", a, g)) for a in range(R_PASSES) for g in (0, 1)], first)
+        interleave_z("gpsimd", 0, "zi0")
         quantize([("z", 0, 0)], zi[0][:], M)
-        for first, count, tag in ((0, 2, "raw23"), (2, 2, "raw01"), (4, 3, "raw11")):
-            held = keep.tile([P, count, M], F32, name="held", tag=tag, align_bytes=64)
-            for n in range(count):
-                gather_skip(first + n, held[:, n, :])
-        unit = PACK * GROUP
-        rounded = {}
-        for g in range(GROUPS):
-            both = keep.tile([P, unit * (1 if g < 1 else 2)], BF16, name="rounded%d" % g, align_bytes=64)
-            rounded[0, g] = both[:, 0:unit]
-            rounded["both", g] = both[:]
-            cast("gpsimd", ("b", 0, g), rounded[0, g])
-        for g in (1, 2, 3):
-            cast("gpsimd", ("b", 1, g), rounded["both", g][:, unit:2 * unit])
-        for g in range(1):
-            rounded[1, g] = keep.tile([P, unit], BF16, name="rounded", tag="act%d" % (1 - g), align_bytes=64)[:]
-            cast("scalar", ("b", 1, g), rounded[1, g])
-        interleave_z(1)
-        wb_sc = keep.tile([P, R_PASSES * H], U8, name="wb_sc", tag="raw02", align_bytes=64)
-
-        def weights_b(g):
-            if g < 1:
-                for a in range(R_PASSES):
-                    quantize([("b", a, g)], rounded[a, g], GROUP, wb_sc[:, g * KP + a * GROUP:g * KP + (a + 1) * GROUP])
-            else:
-                quantize([("b", a, g) for a in range(R_PASSES)], rounded["both", g], GROUP, wb_sc[:, g * KP:(g + 1) * KP])
-
+        quantize(first_keys, first[:], GROUP, "zi0")
+        gathers("first", ("s", 7))
+        third = held("third", [P, 2 * UNIT], BF16, "act1")
+        cast("scalar", ("b", 0, 2), third[:, 0:UNIT])
+        interleave_z("scalar", 1, "zi1")
         quantize([("z", 1, 0)], zi[1][:], M)
-        for g in range(2):
-            weights_b(g)
-            if g == 0:
-                late = keep.tile([P, M], F32, name="late", tag="zi1", align_bytes=64)
-                gather_skip(TILES - 1, late[:])
+        cast("scalar", ("b", 1, 2), third[:, UNIT:2 * UNIT])
+        quantize([("b", a, 2) for a in range(R_PASSES)], third[:], GROUP)
 
         for n in range(PACK):
             pass_a(0, n)
         for n in range(PACK):
-            pass_a(1, n)
             pass_b(0, n)
+        for n in range(PACK):
+            pass_a(1, n)
             pass_b(1, n)
         for n in range(TILES):
-            if n in (1, 3):
-                weights_b(2 + n // 2)
+            if n == 1:
+                last = held("last", [P, 2 * UNIT], BF16, "raw11")
+                quantize(rounded([("scalar", ("b", a, 3)) for a in range(R_PASSES)], last), last[:], GROUP)
             if n >= PACK:
                 for a in range(R_PASSES):
                     pass_a(a, n)

@@ -245,16 +245,16 @@ def tile_list_mural_retouch_advice_kernel(tc, tab_words, tab_scales, offs, pos1,
         fetch_h(1)
         late_units(("gpsimd", 0, 2), ("gpsimd", 1, 2))
         encoder([0, 1], 2)
-        gathers("raw12", ("x", 2), ("x", 3))
+        gathers("raw12", ("x", 2), ("x", 3), ("s", 2))
         late_units(("gpsimd", 2, 2), ("gpsimd", 0, 3))
         encoder([2], 2)
         encoder([0], 3)
-        gathers("raw03", ("s", 2))
+        gathers("raw03", ("s", 3))
         late_units(("gpsimd", 1, 3), ("scalar", 2, 3))
         encoder([1, 2], 3)
         fetch_h(2)
         fetch_h(3)
-        gathers("raw23", ("x", 4), ("x", 5), ("s", 3))
+        gathers("raw23", ("x", 4), ("x", 5))
         gathers("raw02", ("x", 6), ("x", 7))
         silu_gain(0, first_acts[0])
         silu_gain(1, first_acts[1])
@@ -269,12 +269,12 @@ def tile_list_mural_retouch_advice_kernel(tc, tab_words, tab_scales, offs, pos1,
         gathers("raw22", ("s", 4), ("s", 5))
         gathers("raw02", ("s", 6))
 
-        first = held("first", [P, 4 * UNIT], BF16)
+        first = held("first", [P, 4 * UNIT], BF16, "pair")
         first_keys = rounded([("gpsimd", ("b", a, g)) for a in range(R_PASSES) for g in (0, 1)], first)
         interleave_z("gpsimd", 0, "zi0")
         quantize([("z", 0, 0)], zi[0][:], M)
         quantize(first_keys, first[:], GROUP, "zi0")
-        gathers("first", ("s", 7))
+        gathers("pair", ("s", 7))
         third = held("third", [P, 2 * UNIT], BF16, "act1")
         cast("scalar", ("b", 0, 2), third[:, 0:UNIT])
         interleave_z("scalar", 1, "zi1")

@@ -151,14 +151,16 @@ def tile_list_mural_retouch_advice_kernel(tc, tab_words, tab_scales, offs, pos1,
             nc.scalar.activation(zb[b][:, q, :], act, ACT.Copy, scale=gain_sb[:, j:j + 1])
             nc.sync.dma_start(out=zp[b][q * QUAD:(q + 1) * QUAD, :, :], in_=zb[b][:, q, :])
 
-        def interleave_z(engine, b, tag):
+        def interleave_z(b, tag, *shares):
             zi[b] = held("zi", [P, M * PACK], BF16, tag)
-            if engine == "gpsimd":
-                nc.gpsimd.tensor_scalar(zi[b][:].rearrange("p (c t) -> p c t", t=PACK), zp[b][:].rearrange("p t c -> p c t"),
-                                        1.0, 0.0, ALU.mult, ALU.add)
-            else:
-                nc.scalar.copy(out=zi[b][:].rearrange("p (c i t) -> p c t i", i=4, t=PACK),
-                               in_=zp[b][:].rearrange("p t (c i) -> p c t i", i=4))
+            for engine, c0, c1 in shares:
+                dst, src = zi[b][:, c0 * PACK:c1 * PACK], zp[b][:, :, c0:c1]
+                if engine == "gpsimd":
+                    nc.gpsimd.tensor_scalar(dst.rearrange("p (c t) -> p c t", t=PACK), src.rearrange("p t c -> p c t"),
+                                            1.0, 0.0, ALU.mult, ALU.add)
+                else:
+                    nc.scalar.copy(out=dst.rearrange("p (c i t) -> p c t i", i=4, t=PACK),
+                                   in_=src.rearrange("p t (c i) -> p c t i", i=4))
 
         def pass_a(a, n):
             if a == 0:
@@ -271,13 +273,13 @@ def tile_list_mural_retouch_advice_kernel(tc, tab_words, tab_scales, offs, pos1,
 
         first = held("first", [P, 4 * UNIT], BF16, "pair")
         first_keys = rounded([("gpsimd", ("b", a, g)) for a in range(R_PASSES) for g in (0, 1)], first)
-        interleave_z("gpsimd", 0, "zi0")
+        interleave_z(0, "zi0", ("gpsimd", 0, M))
         quantize([("z", 0, 0)], zi[0][:], M)
         quantize(first_keys, first[:], GROUP, "zi0")
         gathers("pair", ("s", 7))
         third = held("third", [P, 2 * UNIT], BF16, "act1")
         cast("scalar", ("b", 0, 2), third[:, 0:UNIT])
-        interleave_z("scalar", 1, "zi1")
+        interleave_z(1, "zi1", ("scalar", 0, M // 2), ("gpsimd", M // 2, M))
         quantize([("z", 1, 0)], zi[1][:], M)
         cast("scalar", ("b", 1, 2), third[:, UNIT:2 * UNIT])
         quantize([("b", a, 2) for a in range(R_PASSES)], third[:], GROUP)

@@ -236,10 +236,9 @@ def tile_list_mural_retouch_advice_kernel(tc, tab_words, tab_scales, offs, pos1,
             early_unit("vector", a, 1)
             encoder([a], 1)
         gathers("raw00", ("x", 0))
-        gathers("raw10", ("x", 1))
         late_units(("scalar", 2, 1))
         encoder([2], 1)
-        first_acts = gathers("raw21", ("s", 0), ("s", 1), spare=2)
+        first_acts = gathers("raw21", ("x", 1), ("s", 0), ("s", 1), spare=2)
         turned = psum.tile([P, P], F32, name="turned", tag="bank")
         nc.tensor.transpose(turned[:], rows[:], ident[:])
         nc.scalar.copy(out=gain_sb[:], in_=turned[:, 0:TILES])

@@ -71,8 +71,7 @@ def tile_list_mural_retouch_advice_kernel(tc, tab_words, tab_scales, offs, pos1,
 
         def cast(engine, key, dst):
             if engine == "gpsimd":
-                nc.gpsimd.tensor_scalar(dst.rearrange("p (c j) -> p c j", j=PACK), raw[key].rearrange("p j c -> p c j"),
-                                        1.0, 0.0, ALU.mult, ALU.add)
+                nc.gpsimd.tensor_copy(dst.rearrange("p (c j) -> p c j", j=PACK), raw[key].rearrange("p j c -> p c j"))
             else:
                 copy = nc.vector.tensor_copy if engine == "vector" else nc.scalar.copy
                 copy(out=dst.rearrange("p (m i j) -> p m j i", i=4, j=PACK),
@@ -156,8 +155,7 @@ def tile_list_mural_retouch_advice_kernel(tc, tab_words, tab_scales, offs, pos1,
             for engine, c0, c1 in shares:
                 dst, src = zi[b][:, c0 * PACK:c1 * PACK], zp[b][:, :, c0:c1]
                 if engine == "gpsimd":
-                    nc.gpsimd.tensor_scalar(dst.rearrange("p (c t) -> p c t", t=PACK), src.rearrange("p t c -> p c t"),
-                                            1.0, 0.0, ALU.mult, ALU.add)
+                    nc.gpsimd.tensor_copy(dst.rearrange("p (c t) -> p c t", t=PACK), src.rearrange("p t c -> p c t"))
                 else:
                     nc.scalar.copy(out=dst.rearrange("p (c i t) -> p c t i", i=4, t=PACK),
                                    in_=src.rearrange("p t (c i) -> p c t i", i=4))

@@ -29,6 +29,7 @@ TILES = H // P
 GROUP = 2 * P
 GROUPS = H // GROUP
 UNIT = PACK * GROUP
+SCALAR_COLUMNS = 5 * M // 8
 
 
 def tile_list_mural_retouch_advice_kernel(tc, tab_words, tab_scales, offs, pos1, pos2, w1, gain,
@@ -141,13 +142,16 @@ def tile_list_mural_retouch_advice_kernel(tc, tab_words, tab_scales, offs, pos1,
         def act_in(tag):
             return held("act", [P, M], F32, tag)[:]
 
-        def silu_gain(j, act):
+        def silu_gain(j, act, engine="scalar"):
             b, q = divmod(j, PACK)
             if q == 0:
                 zb[b] = held("zb%d" % b, [P, PACK, M], BF16, ("big1", None)[b])
                 zp[b] = held("zp", [P, PACK, M], BF16, "raw%d1" % b)
             nc.scalar.activation(act, x[j], ACT.Silu)
-            nc.scalar.activation(zb[b][:, q, :], act, ACT.Copy, scale=gain_sb[:, j:j + 1])
+            if engine == "gpsimd":
+                nc.gpsimd.tensor_scalar(zb[b][:, q, :], act, gain_sb[:, j:j + 1], 0.0, ALU.mult, ALU.add)
+            else:
+                nc.scalar.activation(zb[b][:, q, :], act, ACT.Copy, scale=gain_sb[:, j:j + 1])
             nc.sync.dma_start(out=zp[b][q * QUAD:(q + 1) * QUAD, :, :], in_=zb[b][:, q, :])
 
         def interleave_z(b, tag, *shares):
@@ -263,20 +267,22 @@ def tile_list_mural_retouch_advice_kernel(tc, tab_words, tab_scales, offs, pos1,
         silu_gain(3, act_in("big2"))
         load_w(wb, "b", 0, 2, 2, "big2")
         load_w(wb, "b", 1, 2, 2, "big1")
-        for j, tag in zip(range(PACK, TILES), ("act0", "raw22", "act0", "act1")):
-            silu_gain(j, act_in(tag))
-        gathers("raw22", ("s", 4), ("s", 5))
+        first = held("first", [P, 4 * UNIT], BF16, "pair")
+        silu_gain(4, act_in("act0"), "gpsimd")
+        silu_gain(5, act_in("act1"), "gpsimd")
+        silu_gain(6, act_in("act2"))
+        silu_gain(7, first[:, 3 * UNIT:].bitcast(F32))
+        gathers("raw23", ("s", 4), ("s", 5))
         gathers("raw02", ("s", 6))
 
-        first = held("first", [P, 4 * UNIT], BF16, "pair")
-        first_keys = rounded([("gpsimd", ("b", a, g)) for a in range(R_PASSES) for g in (0, 1)], first)
+        first_keys = rounded([("gpsimd", ("b", 0, 0)), ("gpsimd", ("b", 0, 1)), ("gpsimd", ("b", 1, 0)), ("scalar", ("b", 1, 1))], first)
         interleave_z(0, "zi0", ("gpsimd", 0, M))
         quantize([("z", 0, 0)], zi[0][:], M)
         quantize(first_keys, first[:], GROUP, "zi0")
         gathers("pair", ("s", 7))
-        third = held("third", [P, 2 * UNIT], BF16, "act1")
+        third = held("third", [P, 2 * UNIT], BF16, "act2")
         cast("scalar", ("b", 0, 2), third[:, 0:UNIT])
-        interleave_z(1, "zi1", ("scalar", 0, M // 2), ("gpsimd", M // 2, M))
+        interleave_z(1, "zi1", ("scalar", 0, SCALAR_COLUMNS), ("gpsimd", SCALAR_COLUMNS, M))
         quantize([("z", 1, 0)], zi[1][:], M)
         cast("scalar", ("b", 1, 2), third[:, UNIT:2 * UNIT])
         quantize([("b", a, 2) for a in range(R_PASSES)], third[:], GROUP)

@@ -214,9 +214,11 @@ def tile_list_mural_retouch_advice_kernel(tc, tab_words, tab_scales, offs, pos1,
         nc.sync.dma_start(out=rows[0:TILES, :], in_=gain.rearrange("(n p) -> n p", p=P))
         nc.sync.dma_start(out=rows[TILES:2 * TILES, :], in_=sk.rearrange("(n p) -> n p", p=P))
         nc.sync.dma_start(pos2_sb[:], pos2)
-        for g in (2, 3):
-            for a in range(K_PASSES):
-                load_w1(a, g)
+        load_w1(0, 2)
+        load_w1(1, 2)
+        load_w(w1, "w", 2, 2, 2, "raw23")
+        load_w1(0, 3)
+        load_w1(1, 3)
         load_w(wb, "b", 0, 0, 2, "big0")
         load_w(wb, "b", 1, 0, 2, "wb10")
         for q in range(4):

from contextlib import ExitStack

import concourse.mybir as mybir
from concourse.masks import make_identity

K, T, S, M, H = 1536, 2048, 1024, 512, 1024
FLOPS = 2 * K * H * S + 2 * 2 * H * H * M

F32 = mybir.dt.float32
BF16 = mybir.dt.bfloat16
I32 = mybir.dt.int32
U32 = mybir.dt.uint32
U16 = mybir.dt.uint16
U8 = mybir.dt.uint8
FP8X4 = mybir.dt.float8_e4m3fn_x4
FP4X4 = mybir.dt.float4_e2m1fn_x4
ACT = mybir.ActivationFunctionType
ALU = mybir.AluOpType

P = 128
PACK = 4
KP = P * PACK
BANK = 512
QUAD = 32
K_PASSES = K // KP
R_PASSES = H // KP
HALVES = S // BANK
TILES = H // P
GROUP = 2 * P
GROUPS = H // GROUP
UNIT = PACK * GROUP
SCALAR_COLUMNS = 5 * M // 8


def tile_list_mural_retouch_advice_kernel(tc, tab_words, tab_scales, offs, pos1, pos2, w1, gain,
                                                        wa_words, wa_scales, wb, sk, out):
    nc = tc.nc
    with ExitStack() as ctx:
        keep = ctx.enter_context(tc.tile_pool(name="keep", bufs=1))
        ring = ctx.enter_context(tc.tile_pool(name="ring", bufs=3))
        psum = ctx.enter_context(tc.psum_pool(name="psum", bufs=8))

        def held(name, shape, dtype, tag=None):
            return keep.tile(shape, dtype, name=name, tag=tag or name, align_bytes=64)

        offs_sb = keep.tile([P, S // 16], U16, name="offs_sb")
        pos1_sb = keep.tile([P, M // 16], U16, name="pos1_sb")
        pos2_sb = keep.tile([P, M // 16], U16, name="pos2_sb")
        rows = held("rows", [P, P], F32)
        ident = held("ident", [P, P], F32)
        gain_sb = held("gain_sb", [P, TILES], F32)
        neg_sk = held("neg_sk", [P, TILES], F32)
        tab_sc = held("tab_sc", [P, T // 4], I32)
        wa_sc = held("wa_sc", [P, R_PASSES, H], U8)
        v_sc = held("v_sc", [P, S], U8)
        tab_w, v_w, raw, codes, scales = {}, {}, {}, {}, {}
        acc, h, x, zb, zp, zi, skip, ya, yb, top = {}, {}, {}, {}, {}, {}, {}, {}, {}, {}

        def load_tab(a):
            tab_w[a] = held("tab_w%d" % a, [P, T], I32, "big%d" % a)
            nc.sync.dma_start(out=tab_w[a][:], in_=tab_words[a].rearrange("p t i -> p (t i)").bitcast(I32))

        def load_w(w, name, a, g, groups, tag):
            tile = held("raw", [P, PACK, groups * GROUP], F32, tag)
            nc.sync.dma_start(out=tile[:], in_=w[a * KP:(a + 1) * KP, g * GROUP:(g + groups) * GROUP]
                              .rearrange("(p j) c -> p j c", j=PACK))
            for e in range(groups):
                raw[name, a, g + e] = tile[:, :, e * GROUP:(e + 1) * GROUP]

        def load_w1(a, g):
            load_w(w1, "w", a, g, 1, "raw%d%d" % (a, g))

        def cast(engine, key, dst):
            if engine == "gpsimd":
                nc.gpsimd.tensor_copy(dst.rearrange("p (c j) -> p c j", j=PACK), raw[key].rearrange("p j c -> p c j"))
            else:
                copy = nc.vector.tensor_copy if engine == "vector" else nc.scalar.copy
                copy(out=dst.rearrange("p (m i j) -> p m j i", i=4, j=PACK),
                     in_=raw[key].rearrange("p j (m i) -> p m j i", i=4))

        def quantize(keys, src, width, tag=None):
            n = len(keys) * width
            words = held("codes_%s%d%d" % keys[0], [P, n], U32, tag)
            plane = held("scales_%s%d%d" % keys[0], [P, n], U8)
            nc.vector.quantize_mx(out=words[:].bitcast(FP8X4), scales=plane[:], in_=src)
            for e, key in enumerate(keys):
                codes[key] = words[:, e * width:(e + 1) * width]
                scales[key] = plane[:, e * width:(e + 1) * width]

        def rounded(jobs, dst):
            for e, (engine, key) in enumerate(jobs):
                cast(engine, key, dst[:, e * UNIT:(e + 1) * UNIT])
            return [key for engine, key in jobs]

        def early_unit(engine, a, g):
            grouped = ring.tile([P, UNIT], BF16, name="grouped", tag="grouped", align_bytes=64)
            quantize(rounded([(engine, ("w", a, g))], grouped), grouped[:], GROUP)

        def late_units(*jobs):
            pair = held("pair", [P, len(jobs) * UNIT], BF16)
            quantize(rounded([(engine, ("w", a, g)) for engine, a, g in jobs], pair), pair[:], GROUP)

        def gather_tab(a, pieces):
            v_w[a] = held("v_w%d" % a, [P, S], U32)
            n = S // pieces
            for u in range(pieces):
                nc.vector.tensor_copy(v_w[a][:, u * n:(u + 1) * n],
                                      tab_w[a][:].bitcast(U32).indirect(offs_sb[:, u * n // 16:(u + 1) * n // 16]))

        def encoder_pass(a, j, u):
            if a == 0:
                acc[j, u] = psum.tile([P, BANK], F32, name="acc", tag="bank")
            key, c = ("w", a, j // 2), j % 2
            nc.tensor.matmul_mx(
                out=acc[j, u][:],
                lhsT=codes[key][:, c * P:(c + 1) * P].bitcast(FP8X4),
                lhsT_scale=scales[key][:, c * P:(c + 1) * P],
                rhs=v_w[a][:, u * BANK:(u + 1) * BANK].bitcast(FP8X4),
                rhs_scale=v_sc[4 * a:P, u * BANK:(u + 1) * BANK],
                start=(a == 0), stop=(a == K_PASSES - 1))

        def encoder(passes, g):
            for j in (2 * g, 2 * g + 1):
                for u in range(HALVES):
                    for a in passes:
                        encoder_pass(a, j, u)

        def fetch_h(g):
            for j in (2 * g, 2 * g + 1):
                h[j] = held("h%d" % j, [P, S], F32)
                for u in range(HALVES):
                    nc.scalar.copy(out=h[j][:, u * BANK:(u + 1) * BANK], in_=acc[j, u][:])

        def gathers(tag, *jobs, spare=0):
            dst = held("picked", [P, len(jobs) + spare, M], F32, tag)
            for e, (kind, j) in enumerate(jobs):
                picked, places = (x, pos1_sb) if kind == "x" else (skip, pos2_sb)
                picked[j] = dst[:, e, :]
                nc.vector.tensor_copy(picked[j], h[j][:].indirect(places[:]))
            return [dst[:, e, :] for e in range(len(jobs), len(jobs) + spare)]

        def act_in(tag):
            return held("act", [P, M], F32, tag)[:]

        def silu_gain(j, act, engine="scalar"):
            b, q = divmod(j, PACK)
            if q == 0:
                zb[b] = held("zb%d" % b, [P, PACK, M], BF16, ("big1", None)[b])
                zp[b] = held("zp", [P, PACK, M], BF16, "raw%d1" % b)
            nc.scalar.activation(act, x[j], ACT.Silu)
            if engine == "gpsimd":
                nc.gpsimd.tensor_scalar(zb[b][:, q, :], act, gain_sb[:, j:j + 1], 0.0, ALU.mult, ALU.add)
            else:
                nc.scalar.activation(zb[b][:, q, :], act, ACT.Copy, scale=gain_sb[:, j:j + 1])
            nc.sync.dma_start(out=zp[b][q * QUAD:(q + 1) * QUAD, :, :], in_=zb[b][:, q, :])

        def interleave_z(b, tag, *shares):
            zi[b] = held("zi", [P, M * PACK], BF16, tag)
            for engine, c0, c1 in shares:
                dst, src = zi[b][:, c0 * PACK:c1 * PACK], zp[b][:, :, c0:c1]
                if engine == "gpsimd":
                    nc.gpsimd.tensor_copy(dst.rearrange("p (c t) -> p c t", t=PACK), src.rearrange("p t c -> p c t"))
                else:
                    nc.scalar.copy(out=dst.rearrange("p (c i t) -> p c t i", i=4, t=PACK),
                                   in_=src.rearrange("p t (c i) -> p c t i", i=4))

        def pass_a(a, n):
            if a == 0:
                ya[n] = psum.tile([P, M], F32, name="ya", tag="bank")
                yb[n] = psum.tile([P, M], F32, name="yb", tag="bank")
            z = ("z", a, 0)
            nc.tensor.matmul_mx(
                out=ya[n][:], lhsT=wa_w[:, a, 2 * n * P:2 * (n + 1) * P].bitcast(FP4X4),
                lhsT_scale=wa_sc[:, a, n * P:(n + 1) * P],
                rhs=codes[z].bitcast(FP8X4), rhs_scale=scales[z], start=(a == 0), stop=(a == R_PASSES - 1))

        def pass_b(a, n):
            z = ("z", a, 0)
            key, c = ("b", a, n // 2), n % 2
            nc.tensor.matmul_mx(
                out=yb[n][:], lhsT=codes[key][:, c * P:(c + 1) * P].bitcast(FP8X4),
                lhsT_scale=scales[key][:, c * P:(c + 1) * P],
                rhs=codes[z].bitcast(FP8X4), rhs_scale=scales[z], start=(a == 0), stop=(a == R_PASSES - 1))

        def larger(n):
            ya_sb = ring.tile([P, M], F32, name="ya_sb", tag="ya_sb", bufs=3)
            nc.scalar.copy(out=ya_sb[:], in_=ya[n][:])
            top[n] = ring.tile([P, M], F32, name="top", tag="top", bufs=2)
            nc.vector.tensor_tensor(top[n][:], yb[n][:], ya_sb[:], ALU.max)

        def finish(n, c0=0, c1=M):
            nc.vector.scalar_tensor_tensor(skip[n][:, c0:c1], skip[n][:, c0:c1], neg_sk[:, n:n + 1], top[n][:, c0:c1],
                                           ALU.mult, ALU.add)
            nc.sync.dma_start(out=out[n * P:(n + 1) * P, c0:c1], in_=skip[n][:, c0:c1])

        nc.vector.memset(tab_sc[:], 0)
        nc.vector.memset(wa_sc[:].bitcast(I32), 0)
        nc.vector.memset(rows[:], 0.0)
        make_identity(nc, ident[:])

        nc.sync.dma_start(offs_sb[:], offs)
        load_tab(0)
        load_w1(0, 0)
        for q in range(4):
            nc.sync.dma_start(out=tab_sc[QUAD * q:QUAD * q + 4 * K_PASSES, :],
                              in_=tab_scales[:, 4 * q:4 * q + 4, :].bitcast(I32))
        load_tab(1)
        load_w1(1, 0)
        load_tab(2)
        load_w1(2, 0)
        nc.sync.dma_start(pos1_sb[:], pos1)
        for a in range(K_PASSES):
            load_w1(a, 1)
        nc.sync.dma_start(out=rows[0:TILES, :], in_=gain.rearrange("(n p) -> n p", p=P))
        nc.sync.dma_start(out=rows[TILES:2 * TILES, :], in_=sk.rearrange("(n p) -> n p", p=P))
        nc.sync.dma_start(pos2_sb[:], pos2)
        load_w1(0, 2)
        load_w1(1, 2)
        load_w(w1, "w", 2, 2, 2, "raw23")
        load_w1(0, 3)
        load_w1(1, 3)
        load_w(wb, "b", 0, 0, 2, "big0")
        load_w(wb, "b", 1, 0, 2, "wb10")
        for q in range(4):
            nc.sync.dma_start(out=wa_sc[QUAD * q:QUAD * q + 4, :, :].bitcast(I32),
                              in_=wa_scales[:, 4 * q:4 * q + 4, :].bitcast(I32).rearrange("a r c -> r a c"))

        gather_tab(0, 1)
        nc.vector.tensor_copy(v_sc[:], tab_sc[:].bitcast(U8).indirect(offs_sb[:]))
        early_unit("scalar", 0, 0)
        encoder([0], 0)
        gather_tab(1, 1)
        early_unit("scalar", 1, 0)
        encoder([1], 0)
        gather_tab(2, HALVES)
        early_unit("scalar", 2, 0)
        encoder([2], 0)
        fetch_h(0)
        for a in (0, 1):
            early_unit("vector", a, 1)
            encoder([a], 1)
        gathers("raw00", ("x", 0))
        late_units(("scalar", 2, 1))
        encoder([2], 1)
        first_acts = gathers("raw21", ("x", 1), ("s", 0), ("s", 1), spare=2)
        turned = psum.tile([P, P], F32, name="turned", tag="bank")
        nc.tensor.transpose(turned[:], rows[:], ident[:])
        nc.scalar.copy(out=gain_sb[:], in_=turned[:, 0:TILES])
        nc.scalar.activation(neg_sk[:], turned[:, TILES:2 * TILES], ACT.Copy, scale=-1.0)
        fetch_h(1)
        late_units(("gpsimd", 0, 2), ("gpsimd", 1, 2))
        encoder([0, 1], 2)
        gathers("raw12", ("x", 2), ("x", 3), ("s", 2))
        late_units(("gpsimd", 2, 2), ("gpsimd", 0, 3))
        encoder([2], 2)
        encoder([0], 3)
        gathers("raw03", ("s", 3))
        late_units(("gpsimd", 1, 3), ("scalar", 2, 3))
        encoder([1, 2], 3)
        fetch_h(2)
        fetch_h(3)
        gathers("raw23", ("x", 4), ("x", 5))
        gathers("raw02", ("x", 6), ("x", 7))
        silu_gain(0, first_acts[0])
        silu_gain(1, first_acts[1])
        silu_gain(2, act_in("wa_w"))
        wa_w = held("wa_w", [P, R_PASSES, 2 * H], U8)
        nc.sync.dma_start(out=wa_w[:].bitcast(I32), in_=wa_words.bitcast(I32).rearrange("a p c -> p a c"))
        silu_gain(3, act_in("big2"))
        load_w(wb, "b", 0, 2, 2, "big2")
        load_w(wb, "b", 1, 2, 2, "big1")
        first = held("first", [P, 4 * UNIT], BF16, "pair")
        silu_gain(4, act_in("act0"), "gpsimd")
        silu_gain(5, act_in("act1"), "gpsimd")
        silu_gain(6, act_in("act2"))
        silu_gain(7, first[:, 3 * UNIT:].bitcast(F32))
        gathers("raw23", ("s", 4), ("s", 5))
        gathers("raw02", ("s", 6))

        first_keys = rounded([("gpsimd", ("b", 0, 0)), ("gpsimd", ("b", 0, 1)), ("gpsimd", ("b", 1, 0)), ("scalar", ("b", 1, 1))], first)
        interleave_z(0, "zi0", ("gpsimd", 0, M))
        quantize([("z", 0, 0)], zi[0][:], M)
        quantize(first_keys, first[:], GROUP, "zi0")
        gathers("pair", ("s", 7))
        third = held("third", [P, 2 * UNIT], BF16, "act2")
        cast("scalar", ("b", 0, 2), third[:, 0:UNIT])
        interleave_z(1, "zi1", ("scalar", 0, SCALAR_COLUMNS), ("gpsimd", SCALAR_COLUMNS, M))
        quantize([("z", 1, 0)], zi[1][:], M)
        cast("scalar", ("b", 1, 2), third[:, UNIT:2 * UNIT])
        quantize([("b", a, 2) for a in range(R_PASSES)], third[:], GROUP)

        for n in range(PACK):
            pass_a(0, n)
        for n in range(PACK):
            pass_b(0, n)
        for n in range(PACK):
            pass_a(1, n)
            pass_b(1, n)
        for n in range(TILES):
            if n == 1:
                last = held("last", [P, 2 * UNIT], BF16, "raw11")
                quantize(rounded([("scalar", ("b", a, 3)) for a in range(R_PASSES)], last), last[:], GROUP)
            if n >= PACK:
                for a in range(R_PASSES):
                    pass_a(a, n)
                for a in range(R_PASSES):
                    pass_b(a, n)
            larger(n)
            if n > 0:
                finish(n - 1)
        finish(TILES - 1, 0, M // 2)
        finish(TILES - 1, M // 2, M)
